import numpy as np
import ml_dtypes


def mxq(x, axis, fmt="e4m3"):
    dtype, down = {"e4m3": (ml_dtypes.float8_e4m3fn, 7), "e5m2": (ml_dtypes.float8_e5m2, 14)}[fmt]
    v = np.moveaxis(np.asarray(x, np.float32).astype(ml_dtypes.bfloat16).astype(np.float64), axis, -1)
    blocks = v.reshape(v.shape[:-1] + (-1, 32))
    amax = np.abs(blocks).max(-1, keepdims=True)
    byte = np.maximum(np.where(amax > 0, np.frexp(amax)[1] - 1 + 127, 0) - down, 1)
    scale = np.exp2(byte - 127.0)
    codes = (blocks / scale).astype(np.float32).astype(dtype).astype(np.float64)
    return np.moveaxis((codes * scale).reshape(v.shape), -1, axis)


WIDE = False


def mx_kscale(k):
    if not WIDE:
        return np.ones(k)
    levels = np.array([10, -10, 5, -5, 0])
    if k % 512:
        return np.exp2(np.random.permutation(np.resize(levels, k // 32))).repeat(32)
    a = np.empty((k // 512, 16))
    for p in range(k // 512):
        a[p, :8] = np.random.permutation(np.resize(levels, 8))
        for g in range(8):
            far = levels[np.abs(levels - a[p, g]) >= 10]
            a[p, g + 8] = far[np.random.randint(len(far))]
    return np.exp2(a.ravel()).repeat(32)


def f64(x):
    return np.asarray(x).astype(np.float64)


def striped(idx):
    return np.tile(idx.reshape(-1, 16).T, (8, 1)).astype(np.uint16)


def unstriped(offs):
    return offs[:16].T.reshape(-1).astype(np.int64)


E2M1 = np.array([0.0, 0.5, 1.0, 1.5, 2.0, 3.0, 4.0, 6.0, -0.0, -0.5, -1.0, -1.5, -2.0, -3.0, -4.0, -6.0])


def pack_fp4(w):
    k, n = w.shape
    w = f64(np.asarray(w, np.float32).astype(ml_dtypes.bfloat16)).reshape(k // 32, 32, n)
    amax = np.abs(w).max(1)
    mant, ex = np.frexp(amax / 6.0)
    byte = np.clip(np.where(amax > 0, np.where(mant > 0.5, ex, ex - 1) + 127, 1), 1, 254)
    scaled = (w * np.exp2(127.0 - byte)[:, None, :]).reshape(k, n).astype(np.float32)
    c = np.ascontiguousarray(scaled.reshape(k // 512, 128, 4, n).transpose(0, 1, 3, 2)).astype(ml_dtypes.float4_e2m1fn).view(np.uint8) & 0xF
    words = (c[..., 0::2] | (c[..., 1::2] << 4)).reshape(k // 512, 128, 2 * n)
    return np.ascontiguousarray(words), np.ascontiguousarray(byte.astype(np.uint8).reshape(k // 512, 16, n))


def unpack_fp4(words, scales):
    g, _, n = scales.shape
    words = np.ascontiguousarray(words).reshape(g, 128, n, 2)
    nib = np.empty((g, 128, n, 4), np.uint8)
    nib[..., 0::2] = words & 0xF
    nib[..., 1::2] = words >> 4
    vals = E2M1[nib] * np.repeat(np.exp2(scales.astype(np.float64) - 127.0), 8, axis=1)[..., None]
    return vals.transpose(0, 1, 3, 2).reshape(g * 512, n)


def gelu(v):
    return 0.5 * v * (1.0 + np.tanh(np.sqrt(2.0 / np.pi) * (v + 0.044715 * v**3)))


K, T, S, N, U = 1024, 2048, 1024, 256, 2048
P = 2 ** 7


def setup_inputs():
    n = np.random.standard_normal
    s = mx_kscale(K)[:, None]
    packed_w1 = pack_fp4(n((K, N)) / np.sqrt(K) / s)
    return {
        "xT": (n((K, T)) * s).astype(np.float32),
        "gate": np.tile(np.random.uniform(0.5, 1.5, S), (P, 1)).astype(np.float32),
        "w1_words": packed_w1[0],
        "w1_scales": packed_w1[1],
        "offs": striped(np.random.permutation(T)[:S]),
        "dst": striped(np.random.permutation(U)[:S]),
    }


def reference(xT, gate, w1_words, w1_scales, offs, dst):
    xq = mxq(f64(xT)[:, unstriped(offs)], 0, "e4m3")
    y = gelu(unpack_fp4(w1_words, w1_scales).T @ xq)
    out = np.zeros((N, U))
    out[:, unstriped(dst)] = y * f64(gate)[:1]
    return out

@@ -1,0 +1,159 @@
+from contextlib import ExitStack
+
+import concourse.mybir as mybir
+
+K, T, S, N, U = 1024, 2048, 1024, 256, 2048
+FLOPS = 2 * K * N * S
+
+F32 = mybir.dt.float32
+BF16 = mybir.dt.bfloat16
+I32 = mybir.dt.int32
+U32 = mybir.dt.uint32
+U16 = mybir.dt.uint16
+U8 = mybir.dt.uint8
+FP8X4 = mybir.dt.float8_e4m3fn_x4
+FP4X4 = mybir.dt.float4_e2m1fn_x4
+GELU = mybir.ActivationFunctionType.Gelu_apprx_tanh
+MULT = mybir.AluOpType.mult
+
+P = 128
+PASSES = K // 512
+PER_COL = 16
+BLOCKS = N // P
+
+EARLY_LOADS = ((0, 1024, 0), (1024, 1024, 640))
+FIRST_LOADS = ((0, 1024, 640), (1024, 1024, 640))
+LAST_LOADS = ((0, 1024, 0), (1024, 512, 512), (1536, 256, 256), (1792, 256, 160))
+PIECE = 256
+STRETCHES = ((0, 256, 128), (256, 256, 128), (512, 512, 512))
+
+
+def tile_picked_route2_lingelu_e_kernel(tc, xT, gate, w1_words, w1_scales, offs, dst, out):
+    nc = tc.nc
+    with ExitStack() as ctx:
+        keep = ctx.enter_context(tc.tile_pool(name="keep", bufs=1))
+        psum = ctx.enter_context(tc.psum_pool(name="psum", bufs=1))
+
+        picks = keep.tile([P, S // PER_COL], U16, name="picks")
+        places = keep.tile([P, S // PER_COL], U16, name="places")
+
+        windows = [keep.tile([P, U], F32, name=f"window{b}") for b in range(BLOCKS)]
+        for window in windows:
+            nc.vector.memset(window[:], 0.0)
+
+        w_scales = keep.tile([P, PASSES, N], U8, name="w_scales", align_bytes=64)
+        nc.gpsimd.memset(w_scales[:], 0)
+
+        rows = xT.rearrange("(g p u e) t -> g u p e t", g=PASSES, p=P, u=2, e=2)
+
+        def load_pair(g, u, loads, after_first=None):
+            pairs = keep.tile([P, 2 * T], BF16, name=f"pairs{g}{u}", align_bytes=64)
+            for first, width, by_vector in loads:
+                raw = keep.tile([P, 2, width], F32, name=f"raw{g}{u}_{first}", align_bytes=64)
+                nc.sync.dma_start(out=raw[:], in_=rows[g, u, :, :, first : first + width])
+                if after_first is not None and first == 0:
+                    after_first()
+                for lo, hi, cast in ((0, by_vector, nc.vector.tensor_copy), (by_vector, width, nc.scalar.copy)):
+                    if hi > lo:
+                        cast(
+                            pairs[:, 2 * (first + lo) : 2 * (first + hi)].rearrange("p (c i e) -> p c e i", i=4, e=2),
+                            raw[:, :, lo:hi].rearrange("p e (c i) -> p c e i", i=4),
+                        )
+            return pairs[:].bitcast(U32)
+
+        def load_lists():
+            nc.sync.dma_start(picks[:], offs)
+            nc.sync.dma_start(places[:], dst)
+            for q in range(4):
+                nc.sync.dma_start(
+                    out=w_scales[32 * q : 32 * q + 4].bitcast(I32),
+                    in_=w1_scales.bitcast(I32)[:, 4 * q : 4 * q + 4, :].rearrange("g r n -> r g n"),
+                )
+
+        codes = [keep.tile([P, S], U32, name=f"codes{g}", align_bytes=64) for g in range(PASSES)]
+        scales = [keep.tile([P, S], U8, name=f"scales{g}", align_bytes=64) for g in range(PASSES)]
+
+        woven0 = keep.tile([P, S, 2], U32, name="woven0", align_bytes=64)
+        for u in range(2):
+            words = load_pair(0, u, FIRST_LOADS if u == 0 else EARLY_LOADS, load_lists if u == 0 else None)
+            nc.vector.tensor_copy(woven0[:, :, u], words.indirect(picks[:]))
+        nc.vector.quantize_mx(
+            out=codes[0][:].bitcast(FP8X4),
+            scales=scales[0][:],
+            in_=woven0[:].rearrange("p s u -> p (s u)").bitcast(BF16),
+        )
+
+        woven1 = [keep.tile([P, PIECE, 2], U32, name=f"woven1_{c}", align_bytes=64) for c in range(S // PIECE)]
+        halves = {c: keep.tile([P, 2, PIECE], U32, name=f"halves{c}", align_bytes=64) for c in range(1, S // PIECE)}
+
+        def gather_piece(words, c, u):
+            cols = slice(c * PIECE // PER_COL, (c + 1) * PIECE // PER_COL)
+            target = halves[c][:, u, :] if c in halves else woven1[c][:, :, u]
+            nc.vector.tensor_copy(target, words.indirect(picks[:, cols]))
+
+        words = load_pair(1, 0, EARLY_LOADS)
+        for c in range(S // PIECE):
+            gather_piece(words, c, 0)
+        words = load_pair(1, 1, LAST_LOADS)
+
+        w_words = keep.tile([P, PASSES, 2 * N], U8, name="w_words", align_bytes=64)
+        nc.sync.dma_start(out=w_words[:].bitcast(I32), in_=w1_words.bitcast(I32).rearrange("g p n -> p g n"))
+        gates = []
+        for first, width, n_cols in STRETCHES:
+            gate_sb = keep.tile([P, width], F32, name=f"gate{first}")
+            nc.sync.dma_start(out=gate_sb[:], in_=gate[:, first : first + width])
+            gates.append(gate_sb)
+
+        def finish_piece(c):
+            gather_piece(words, c, 1)
+            if c in halves:
+                nc.scalar.copy(
+                    woven1[c][:].rearrange("p (c i) u -> p c u i", i=4),
+                    halves[c][:].rearrange("p u (c i) -> p c u i", i=4),
+                )
+            nc.vector.quantize_mx(
+                out=codes[1][:, c * PIECE : (c + 1) * PIECE].bitcast(FP8X4),
+                scales=scales[1][:, c * PIECE : (c + 1) * PIECE],
+                in_=woven1[c][:].rearrange("p s u -> p (s u)").bitcast(BF16),
+            )
+
+        def product(acc, b, entries):
+            for g in range(PASSES):
+                nc.tensor.matmul_mx(
+                    out=acc,
+                    lhsT=w_words[:, g, 2 * P * b : 2 * P * (b + 1)].bitcast(FP4X4),
+                    lhsT_scale=w_scales[:, g, P * b : P * (b + 1)],
+                    rhs=codes[g][:, entries].bitcast(FP8X4),
+                    rhs_scale=scales[g][:, entries],
+                    start=(g == 0),
+                    stop=(g == PASSES - 1),
+                )
+
+        def finish_stretch(j, b):
+            first, width, n_cols = STRETCHES[j]
+            y = keep.tile([P, width], F32, name=f"y{first}_{b}")
+            if j == 0 and b == 0:
+                for lo in range(0, width, n_cols):
+                    acc = psum.tile([P, n_cols], F32, name=f"acc_first{lo}")
+                    product(acc[:], b, slice(first + lo, first + lo + n_cols))
+                    nc.scalar.activation(y[:, lo : lo + n_cols], acc[:], GELU)
+            else:
+                acc = psum.tile([P, width], F32, name=f"acc{first}_{b}")
+                for lo in range(0, width, n_cols):
+                    product(acc[:, lo : lo + n_cols], b, slice(first + lo, first + lo + n_cols))
+                nc.scalar.activation(y[:], acc[:], GELU)
+            cols = slice(first // PER_COL, (first + width) // PER_COL)
+            nc.vector.tensor_tensor(windows[b][:].indirect(places[:, cols]), y[:], gates[j][:], MULT)
+
+        finish_piece(0)
+        finish_piece(1)
+        finish_stretch(0, 0)
+        finish_piece(2)
+        finish_piece(3)
+        finish_stretch(0, 1)
+        for j in (1, 2):
+            for b in range(BLOCKS):
+                finish_stretch(j, b)
+
+        for b in range(BLOCKS):
+            nc.sync.dma_start(out=out[P * b : P * (b + 1), :], in_=windows[b][:])

@@ -21,9 +21,12 @@ PASSES = K // 512
 PER_COL = 16
 BLOCKS = N // P
 
-EARLY_LOADS = ((0, 1024, 0), (1024, 1024, 640))
-FIRST_LOADS = ((0, 1024, 640), (1024, 1024, 640))
-LAST_LOADS = ((0, 1024, 0), (1024, 512, 512), (1536, 256, 256), (1792, 256, 160))
+LOADS = (
+    ((0, 1024, 672), (1024, 1024, 672)),
+    ((0, 1024, 0), (1024, 1024, 672)),
+    ((0, 1024, 0), (1024, 1024, 448)),
+    ((0, 640, 0), (640, 640, 0), (1280, 512, 384), (1792, 256, 160)),
+)
 PIECE = 256
 STRETCHES = ((0, 256, 128), (256, 256, 128), (512, 512, 512))
 
@@ -40,6 +43,10 @@ def tile_picked_route2_lingelu_e_kernel(tc, xT, gate, w1_words, w1_scales, offs,
         windows = [keep.tile([P, U], F32, name=f"window{b}") for b in range(BLOCKS)]
         for window in windows:
             nc.vector.memset(window[:], 0.0)
+
+        warm = keep.tile([P, 16], F32, name="warm")
+        nc.gpsimd.memset(warm[:, 0:8], 0.0)
+        nc.scalar.activation(warm[:, 8:16], warm[:, 0:8], GELU)
 
         w_scales = keep.tile([P, PASSES, N], U8, name="w_scales", align_bytes=64)
         nc.gpsimd.memset(w_scales[:], 0)
@@ -61,21 +68,15 @@ def tile_picked_route2_lingelu_e_kernel(tc, xT, gate, w1_words, w1_scales, offs,
                         )
             return pairs[:].bitcast(U32)
 
-        def load_lists():
+        def load_picks():
             nc.sync.dma_start(picks[:], offs)
-            nc.sync.dma_start(places[:], dst)
-            for q in range(4):
-                nc.sync.dma_start(
-                    out=w_scales[32 * q : 32 * q + 4].bitcast(I32),
-                    in_=w1_scales.bitcast(I32)[:, 4 * q : 4 * q + 4, :].rearrange("g r n -> r g n"),
-                )
 
         codes = [keep.tile([P, S], U32, name=f"codes{g}", align_bytes=64) for g in range(PASSES)]
         scales = [keep.tile([P, S], U8, name=f"scales{g}", align_bytes=64) for g in range(PASSES)]
 
         woven0 = keep.tile([P, S, 2], U32, name="woven0", align_bytes=64)
         for u in range(2):
-            words = load_pair(0, u, FIRST_LOADS if u == 0 else EARLY_LOADS, load_lists if u == 0 else None)
+            words = load_pair(0, u, LOADS[u], load_picks if u == 0 else None)
             nc.vector.tensor_copy(woven0[:, :, u], words.indirect(picks[:]))
         nc.vector.quantize_mx(
             out=codes[0][:].bitcast(FP8X4),
@@ -91,13 +92,19 @@ def tile_picked_route2_lingelu_e_kernel(tc, xT, gate, w1_words, w1_scales, offs,
             target = halves[c][:, u, :] if c in halves else woven1[c][:, :, u]
             nc.vector.tensor_copy(target, words.indirect(picks[:, cols]))
 
-        words = load_pair(1, 0, EARLY_LOADS)
+        words = load_pair(1, 0, LOADS[2])
         for c in range(S // PIECE):
             gather_piece(words, c, 0)
-        words = load_pair(1, 1, LAST_LOADS)
+        words = load_pair(1, 1, LOADS[3])
 
         w_words = keep.tile([P, PASSES, 2 * N], U8, name="w_words", align_bytes=64)
         nc.sync.dma_start(out=w_words[:].bitcast(I32), in_=w1_words.bitcast(I32).rearrange("g p n -> p g n"))
+        for q in range(4):
+            nc.sync.dma_start(
+                out=w_scales[32 * q : 32 * q + 4].bitcast(I32),
+                in_=w1_scales.bitcast(I32)[:, 4 * q : 4 * q + 4, :].rearrange("g r n -> r g n"),
+            )
+        nc.sync.dma_start(places[:], dst)
         gates = []
         for first, width, n_cols in STRETCHES:
             gate_sb = keep.tile([P, width], F32, name=f"gate{first}")

@@ -14,21 +14,23 @@ U8 = mybir.dt.uint8
 FP8X4 = mybir.dt.float8_e4m3fn_x4
 FP4X4 = mybir.dt.float4_e2m1fn_x4
 GELU = mybir.ActivationFunctionType.Gelu_apprx_tanh
+COPY = mybir.ActivationFunctionType.Copy
 MULT = mybir.AluOpType.mult
 
 P = 128
 PASSES = K // 512
 PER_COL = 16
 BLOCKS = N // P
+HALF = T // 2
 
-LOADS = (
-    ((0, 1024, 672), (1024, 1024, 672)),
-    ((0, 1024, 0), (1024, 1024, 672)),
-    ((0, 1024, 0), (1024, 1024, 448)),
-    ((0, 640, 0), (640, 640, 0), (1280, 512, 384), (1792, 256, 160)),
-)
+PAIR_SHARES = ((672, 672), (0, 704), (0, 400))
+ROW_SHARES = ((0, 0), (0, 0))
 PIECE = 256
-STRETCHES = ((0, 256, 128), (256, 256, 128), (512, 512, 512))
+N_COLS = 128
+HALF_PIECE = PIECE // 2
+LOWER = {c: HALF_PIECE + (c - 1) * PIECE for c in (1, 2, 3)}
+UPPER = {c: LOWER[3] + PIECE + (3 - c) * HALF_PIECE for c in (1, 2, 3)}
+STAGE = 2 * UPPER[1] - LOWER[1]
 
 
 def tile_picked_route2_lingelu_e_kernel(tc, xT, gate, w1_words, w1_scales, offs, dst, out):
@@ -50,17 +52,26 @@ def tile_picked_route2_lingelu_e_kernel(tc, xT, gate, w1_words, w1_scales, offs,
 
         w_scales = keep.tile([P, PASSES, N], U8, name="w_scales", align_bytes=64)
         nc.gpsimd.memset(w_scales[:], 0)
+        for q in range(4):
+            nc.gpsimd.dma_start(
+                out=w_scales[32 * q : 32 * q + 4].bitcast(I32),
+                in_=w1_scales.bitcast(I32)[:, 4 * q : 4 * q + 4, :].rearrange("g r n -> r g n"),
+            )
 
-        rows = xT.rearrange("(g p u e) t -> g u p e t", g=PASSES, p=P, u=2, e=2)
+        pair_rows = xT.rearrange("(g p u e) t -> g u p e t", g=PASSES, p=P, u=2, e=2)
+        single_rows = xT.rearrange("(g p j) t -> g j p t", g=PASSES, p=P, j=4)
 
-        def load_pair(g, u, loads, after_first=None):
+        def entry_cols(c, pieces=1):
+            return slice(c * PIECE // PER_COL, (c + pieces) * PIECE // PER_COL)
+
+        def load_pair(g, u, shares):
             pairs = keep.tile([P, 2 * T], BF16, name=f"pairs{g}{u}", align_bytes=64)
-            for first, width, by_vector in loads:
-                raw = keep.tile([P, 2, width], F32, name=f"raw{g}{u}_{first}", align_bytes=64)
-                nc.sync.dma_start(out=raw[:], in_=rows[g, u, :, :, first : first + width])
-                if after_first is not None and first == 0:
-                    after_first()
-                for lo, hi, cast in ((0, by_vector, nc.vector.tensor_copy), (by_vector, width, nc.scalar.copy)):
+            for first, by_vector in zip((0, HALF), shares):
+                raw = keep.tile([P, 2, HALF], F32, name=f"raw{g}{u}_{first}", align_bytes=64)
+                nc.sync.dma_start(out=raw[:], in_=pair_rows[g, u, :, :, first : first + HALF])
+                if (g, u, first) == (0, 0, 0):
+                    nc.sync.dma_start(picks[:], offs)
+                for lo, hi, cast in ((0, by_vector, nc.vector.tensor_copy), (by_vector, HALF, nc.scalar.copy)):
                     if hi > lo:
                         cast(
                             pairs[:, 2 * (first + lo) : 2 * (first + hi)].rearrange("p (c i e) -> p c e i", i=4, e=2),
@@ -68,99 +79,143 @@ def tile_picked_route2_lingelu_e_kernel(tc, xT, gate, w1_words, w1_scales, offs,
                         )
             return pairs[:].bitcast(U32)
 
-        def load_picks():
-            nc.sync.dma_start(picks[:], offs)
+        def load_row(j, shares):
+            raw = keep.tile([P, T], F32, name=f"row{j}", align_bytes=64)
+            rounded = keep.tile([P, T], BF16, name=f"rounded{j}", align_bytes=64)
+            for first, by_vector in zip((0, HALF), shares):
+                nc.sync.dma_start(out=raw[:, first : first + HALF], in_=single_rows[1, j, :, first : first + HALF])
+                for lo, hi, cast in ((0, by_vector, nc.vector.tensor_copy), (by_vector, HALF, nc.scalar.copy)):
+                    if hi > lo:
+                        cast(rounded[:, first + lo : first + hi], raw[:, first + lo : first + hi])
+            return raw, rounded
 
-        codes = [keep.tile([P, S], U32, name=f"codes{g}", align_bytes=64) for g in range(PASSES)]
-        scales = [keep.tile([P, S], U8, name=f"scales{g}", align_bytes=64) for g in range(PASSES)]
+        def quantise(name, count, woven):
+            codes = keep.tile([P, count], U32, name=f"codes{name}", align_bytes=64)
+            scales = keep.tile([P, count], U8, name=f"scales{name}", align_bytes=64)
+            nc.vector.quantize_mx(
+                out=codes[:].bitcast(FP8X4),
+                scales=scales[:],
+                in_=woven.bitcast(BF16),
+            )
+            return codes, scales
 
         woven0 = keep.tile([P, S, 2], U32, name="woven0", align_bytes=64)
         for u in range(2):
-            words = load_pair(0, u, LOADS[u], load_picks if u == 0 else None)
+            words = load_pair(0, u, PAIR_SHARES[u])
             nc.vector.tensor_copy(woven0[:, :, u], words.indirect(picks[:]))
-        nc.vector.quantize_mx(
-            out=codes[0][:].bitcast(FP8X4),
-            scales=scales[0][:],
-            in_=woven0[:].rearrange("p s u -> p (s u)").bitcast(BF16),
-        )
+        pass0 = quantise("_pass0", S, woven0[:].rearrange("p s u -> p (s u)"))
+        pass1 = {}
 
-        woven1 = [keep.tile([P, PIECE, 2], U32, name=f"woven1_{c}", align_bytes=64) for c in range(S // PIECE)]
-        halves = {c: keep.tile([P, 2, PIECE], U32, name=f"halves{c}", align_bytes=64) for c in range(1, S // PIECE)}
+        words = load_pair(1, 0, PAIR_SHARES[2])
+        stage = keep.tile([P, STAGE], U32, name="stage", align_bytes=64)
+        lead = stage[:, LOWER[3] : LOWER[3] + 2 * PIECE]
+        lead_rows = lead.bitcast(BF16).rearrange("p (s j) -> p s j", j=4)
+        lead_picks = picks[:, entry_cols(0)]
+        nc.vector.tensor_copy(lead.rearrange("p (s u) -> p s u", u=2)[:, :, 0], words.indirect(lead_picks))
 
-        def gather_piece(words, c, u):
-            cols = slice(c * PIECE // PER_COL, (c + 1) * PIECE // PER_COL)
-            target = halves[c][:, u, :] if c in halves else woven1[c][:, :, u]
-            nc.vector.tensor_copy(target, words.indirect(picks[:, cols]))
+        def gather_words(c):
+            nc.vector.tensor_copy(stage[:, LOWER[c] : LOWER[c] + PIECE], words.indirect(picks[:, entry_cols(c)]))
 
-        words = load_pair(1, 0, LOADS[2])
-        for c in range(S // PIECE):
-            gather_piece(words, c, 0)
-        words = load_pair(1, 1, LOADS[3])
+        gather_words(1)
+        gather_words(2)
+        raw2, rounded2 = load_row(2, ROW_SHARES[0])
+        nc.vector.tensor_copy(lead_rows[:, :, 2], raw2[:].indirect(lead_picks))
+        raw3, rounded3 = load_row(3, ROW_SHARES[1])
 
         w_words = keep.tile([P, PASSES, 2 * N], U8, name="w_words", align_bytes=64)
         nc.sync.dma_start(out=w_words[:].bitcast(I32), in_=w1_words.bitcast(I32).rearrange("g p n -> p g n"))
-        for q in range(4):
-            nc.sync.dma_start(
-                out=w_scales[32 * q : 32 * q + 4].bitcast(I32),
-                in_=w1_scales.bitcast(I32)[:, 4 * q : 4 * q + 4, :].rearrange("g r n -> r g n"),
-            )
         nc.sync.dma_start(places[:], dst)
-        gates = []
-        for first, width, n_cols in STRETCHES:
-            gate_sb = keep.tile([P, width], F32, name=f"gate{first}")
-            nc.sync.dma_start(out=gate_sb[:], in_=gate[:, first : first + width])
-            gates.append(gate_sb)
+        gate_tiles = []
+        for first, count in ((0, PIECE), (PIECE, PIECE), (2 * PIECE, 2 * PIECE)):
+            gate_sb = keep.tile([P, count], F32, name=f"gate{first}")
+            nc.sync.dma_start(out=gate_sb[:], in_=gate[:, first : first + count])
+            gate_tiles.append(gate_sb)
+        gates = [gate_tiles[0][:], gate_tiles[1][:], gate_tiles[2][:, 0:PIECE], gate_tiles[2][:, PIECE : 2 * PIECE]]
 
-        def finish_piece(c):
-            gather_piece(words, c, 1)
-            if c in halves:
-                nc.scalar.copy(
-                    woven1[c][:].rearrange("p (c i) u -> p c u i", i=4),
-                    halves[c][:].rearrange("p u (c i) -> p c u i", i=4),
-                )
-            nc.vector.quantize_mx(
-                out=codes[1][:, c * PIECE : (c + 1) * PIECE].bitcast(FP8X4),
-                scales=scales[1][:, c * PIECE : (c + 1) * PIECE],
-                in_=woven1[c][:].rearrange("p s u -> p (s u)").bitcast(BF16),
-            )
+        def weave(c):
+            upper = stage[:, UPPER[c] : UPPER[c] + PIECE].bitcast(BF16).rearrange("p (s e) -> p s e", e=2)
+            for e, rounded in enumerate((rounded2, rounded3)):
+                nc.scalar.activation(upper[:, :, e], rounded[:].indirect(picks[:, entry_cols(c)]), COPY)
+            both = stage[:, LOWER[c] : 2 * UPPER[c] - LOWER[c]].rearrange("p (u r) -> p u r", u=2)
+            source = both[:, :, 0:PIECE].rearrange("p u (h c i) -> p h c u i", h=2, i=4)
+            woven = keep.tile([P, 2 * PIECE], U32, name=f"woven1_{c}", align_bytes=64)
+            target = woven[:].rearrange("p (h c i u) -> p h c u i", h=2, i=4, u=2)
+            for h in range(2):
+                nc.scalar.copy(target[:, h], source[:, h])
+            return woven[:]
 
-        def product(acc, b, entries):
-            for g in range(PASSES):
+        def behind_weave(c, width=PIECE):
+            first = LOWER[c] - HALF_PIECE
+            return stage[:, first : first + width].bitcast(F32)
+
+        def product(acc, c, b, lo):
+            for g, (codes, scales), start in ((0, pass0, c * PIECE + lo), (1, pass1[c], lo)):
+                entries = slice(start, start + N_COLS)
                 nc.tensor.matmul_mx(
                     out=acc,
                     lhsT=w_words[:, g, 2 * P * b : 2 * P * (b + 1)].bitcast(FP4X4),
                     lhsT_scale=w_scales[:, g, P * b : P * (b + 1)],
-                    rhs=codes[g][:, entries].bitcast(FP8X4),
-                    rhs_scale=scales[g][:, entries],
+                    rhs=codes[:, entries].bitcast(FP8X4),
+                    rhs_scale=scales[:, entries],
                     start=(g == 0),
                     stop=(g == PASSES - 1),
                 )
 
-        def finish_stretch(j, b):
-            first, width, n_cols = STRETCHES[j]
-            y = keep.tile([P, width], F32, name=f"y{first}_{b}")
-            if j == 0 and b == 0:
-                for lo in range(0, width, n_cols):
-                    acc = psum.tile([P, n_cols], F32, name=f"acc_first{lo}")
-                    product(acc[:], b, slice(first + lo, first + lo + n_cols))
-                    nc.scalar.activation(y[:, lo : lo + n_cols], acc[:], GELU)
-            else:
-                acc = psum.tile([P, width], F32, name=f"acc{first}_{b}")
-                for lo in range(0, width, n_cols):
-                    product(acc[:, lo : lo + n_cols], b, slice(first + lo, first + lo + n_cols))
-                nc.scalar.activation(y[:], acc[:], GELU)
-            cols = slice(first // PER_COL, (first + width) // PER_COL)
-            nc.vector.tensor_tensor(windows[b][:].indirect(places[:, cols]), y[:], gates[j][:], MULT)
+        def multiply(acc, c, b):
+            for lo in range(0, PIECE, N_COLS):
+                product(acc[:, lo : lo + N_COLS], c, b, lo)
+            return acc
 
-        finish_piece(0)
-        finish_piece(1)
-        finish_stretch(0, 0)
-        finish_piece(2)
-        finish_piece(3)
-        finish_stretch(0, 1)
-        for j in (1, 2):
-            for b in range(BLOCKS):
-                finish_stretch(j, b)
+        def bank(name, width=PIECE):
+            acc = psum.tile([P, width], F32, name=name)
+            return acc[:]
+
+        def scatter(c, b, y, gate_ap, pieces=1):
+            nc.vector.tensor_tensor(windows[b][:].indirect(places[:, entry_cols(c, pieces)]), y, gate_ap, MULT)
+
+        def result_tile(name):
+            y = keep.tile([P, PIECE], F32, name=name)
+            return y[:]
+
+        nc.vector.tensor_copy(lead_rows[:, :, 3], raw3[:].indirect(lead_picks))
+        pass1[0] = quantise("0", PIECE, lead)
+        gather_words(3)
+        y00 = result_tile("y00")
+        for lo in range(0, PIECE, N_COLS):
+            acc = bank(f"acc_first{lo}", N_COLS)
+            product(acc, 0, 0, lo)
+            nc.scalar.activation(y00[:, lo : lo + N_COLS], acc, GELU)
+        acc01 = multiply(bank("acc01"), 0, 1)
+        scatter(0, 0, y00, gates[0])
+
+        pass1[1] = quantise("1", PIECE, weave(1))
+        y01 = behind_weave(1)
+        nc.scalar.activation(y01, acc01, GELU)
+        scatter(0, 1, y01, gates[0])
+        y10 = result_tile("y10")
+        nc.scalar.activation(y10, multiply(bank("acc10"), 1, 0), GELU)
+        acc11 = multiply(bank("acc11"), 1, 1)
+        scatter(1, 0, y10, gates[1])
+
+        pass1[2] = quantise("2", PIECE, weave(2))
+        y11 = behind_weave(2)
+        nc.scalar.activation(y11, acc11, GELU)
+        scatter(1, 1, y11, gates[1])
+        acc20 = multiply(bank("acc20"), 2, 0)
+        acc_last = bank("acc_last", 2 * PIECE)
+        multiply(acc_last[:, 0:PIECE], 2, 1)
+
+        pass1[3] = quantise("3", PIECE, weave(3))
+        y20 = behind_weave(3)
+        nc.scalar.activation(y20, acc20, GELU)
+        scatter(2, 0, y20, gates[2])
+        y30 = result_tile("y30")
+        nc.scalar.activation(y30, multiply(bank("acc30"), 3, 0), GELU)
+        multiply(acc_last[:, PIECE : 2 * PIECE], 3, 1)
+        scatter(3, 0, y30, gates[3])
+        y_last = behind_weave(3, 2 * PIECE)
+        nc.scalar.activation(y_last, acc_last, GELU)
+        scatter(2, 1, y_last, gate_tiles[2][:], 2)
 
         for b in range(BLOCKS):
             nc.sync.dma_start(out=out[P * b : P * (b + 1), :], in_=windows[b][:])

@@ -16,6 +16,7 @@ FP4X4 = mybir.dt.float4_e2m1fn_x4
 GELU = mybir.ActivationFunctionType.Gelu_apprx_tanh
 COPY = mybir.ActivationFunctionType.Copy
 MULT = mybir.AluOpType.mult
+ADD = mybir.AluOpType.add
 
 P = 128
 PASSES = K // 512
@@ -23,8 +24,12 @@ PER_COL = 16
 BLOCKS = N // P
 HALF = T // 2
 
-PAIR_SHARES = ((672, 672), (0, 704), (0, 400))
-ROW_SHARES = ((0, 0), (0, 0))
+PAIR_LOADS = (
+    ((0, 1024, "vector", 672), (1024, 1024, "vector", 672)),
+    ((0, 1024, "gpsimd", 384), (1024, 1024, "vector", 704)),
+    ((0, 1024, "gpsimd", 384), (1024, 512, "vector", 0), (1536, 512, "vector", 0)),
+)
+ROW_SHARES = ((0, 0), (1024, 512))
 PIECE = 256
 N_COLS = 128
 HALF_PIECE = PIECE // 2
@@ -64,14 +69,19 @@ def tile_picked_route2_lingelu_e_kernel(tc, xT, gate, w1_words, w1_scales, offs,
         def entry_cols(c, pieces=1):
             return slice(c * PIECE // PER_COL, (c + pieces) * PIECE // PER_COL)
 
-        def load_pair(g, u, shares):
+        def gpsimd_round(target, source):
+            nc.gpsimd.tensor_scalar(target, source, 1.0, 0.0, MULT, ADD)
+
+        helpers = {"vector": nc.vector.tensor_copy, "gpsimd": gpsimd_round}
+
+        def load_pair(g, u, loads):
             pairs = keep.tile([P, 2 * T], BF16, name=f"pairs{g}{u}", align_bytes=64)
-            for first, by_vector in zip((0, HALF), shares):
-                raw = keep.tile([P, 2, HALF], F32, name=f"raw{g}{u}_{first}", align_bytes=64)
-                nc.sync.dma_start(out=raw[:], in_=pair_rows[g, u, :, :, first : first + HALF])
+            for first, width, helper, by_helper in loads:
+                raw = keep.tile([P, 2, width], F32, name=f"raw{g}{u}_{first}", align_bytes=64)
+                nc.sync.dma_start(out=raw[:], in_=pair_rows[g, u, :, :, first : first + width])
                 if (g, u, first) == (0, 0, 0):
                     nc.sync.dma_start(picks[:], offs)
-                for lo, hi, cast in ((0, by_vector, nc.vector.tensor_copy), (by_vector, HALF, nc.scalar.copy)):
+                for lo, hi, cast in ((0, by_helper, helpers[helper]), (by_helper, width, nc.scalar.copy)):
                     if hi > lo:
                         cast(
                             pairs[:, 2 * (first + lo) : 2 * (first + hi)].rearrange("p (c i e) -> p c e i", i=4, e=2),
@@ -82,15 +92,15 @@ def tile_picked_route2_lingelu_e_kernel(tc, xT, gate, w1_words, w1_scales, offs,
         def load_row(j, shares):
             raw = keep.tile([P, T], F32, name=f"row{j}", align_bytes=64)
             rounded = keep.tile([P, T], BF16, name=f"rounded{j}", align_bytes=64)
-            for first, by_vector in zip((0, HALF), shares):
+            for first, by_gpsimd in zip((0, HALF), shares):
                 nc.sync.dma_start(out=raw[:, first : first + HALF], in_=single_rows[1, j, :, first : first + HALF])
-                for lo, hi, cast in ((0, by_vector, nc.vector.tensor_copy), (by_vector, HALF, nc.scalar.copy)):
+                for lo, hi, cast in ((0, by_gpsimd, gpsimd_round), (by_gpsimd, HALF, nc.scalar.copy)):
                     if hi > lo:
                         cast(rounded[:, first + lo : first + hi], raw[:, first + lo : first + hi])
             return raw, rounded
 
         def quantise(name, count, woven):
-            codes = keep.tile([P, count], U32, name=f"codes{name}", align_bytes=64)
+            codes = keep.tile([P, count], U32, name=f"codes{name}", tag=f"codes{name}", align_bytes=64)
             scales = keep.tile([P, count], U8, name=f"scales{name}", align_bytes=64)
             nc.vector.quantize_mx(
                 out=codes[:].bitcast(FP8X4),
@@ -101,12 +111,12 @@ def tile_picked_route2_lingelu_e_kernel(tc, xT, gate, w1_words, w1_scales, offs,
 
         woven0 = keep.tile([P, S, 2], U32, name="woven0", align_bytes=64)
         for u in range(2):
-            words = load_pair(0, u, PAIR_SHARES[u])
+            words = load_pair(0, u, PAIR_LOADS[u])
             nc.vector.tensor_copy(woven0[:, :, u], words.indirect(picks[:]))
         pass0 = quantise("_pass0", S, woven0[:].rearrange("p s u -> p (s u)"))
         pass1 = {}
 
-        words = load_pair(1, 0, PAIR_SHARES[2])
+        words = load_pair(1, 0, PAIR_LOADS[2])
         stage = keep.tile([P, STAGE], U32, name="stage", align_bytes=64)
         lead = stage[:, LOWER[3] : LOWER[3] + 2 * PIECE]
         lead_rows = lead.bitcast(BF16).rearrange("p (s j) -> p s j", j=4)
@@ -138,7 +148,7 @@ def tile_picked_route2_lingelu_e_kernel(tc, xT, gate, w1_words, w1_scales, offs,
                 nc.scalar.activation(upper[:, :, e], rounded[:].indirect(picks[:, entry_cols(c)]), COPY)
             both = stage[:, LOWER[c] : 2 * UPPER[c] - LOWER[c]].rearrange("p (u r) -> p u r", u=2)
             source = both[:, :, 0:PIECE].rearrange("p u (h c i) -> p h c u i", h=2, i=4)
-            woven = keep.tile([P, 2 * PIECE], U32, name=f"woven1_{c}", align_bytes=64)
+            woven = keep.tile([P, 2 * PIECE], U32, name=f"woven1_{c}", tag="codes0" if c == 1 else f"woven{c}", align_bytes=64)
             target = woven[:].rearrange("p (h c i u) -> p h c u i", h=2, i=4, u=2)
             for h in range(2):
                 nc.scalar.copy(target[:, h], source[:, h])
@@ -166,9 +176,15 @@ def tile_picked_route2_lingelu_e_kernel(tc, xT, gate, w1_words, w1_scales, offs,
                 product(acc[:, lo : lo + N_COLS], c, b, lo)
             return acc
 
-        def bank(name, width=PIECE):
-            acc = psum.tile([P, width], F32, name=name)
+        def bank(name, tag, width=PIECE):
+            acc = psum.tile([P, width], F32, name=name, tag=tag)
             return acc[:]
+
+        def first_block(c, y):
+            for lo in range(0, PIECE, N_COLS):
+                acc = bank(f"acc{c}_{lo}", f"first{lo}", N_COLS)
+                product(acc, c, 0, lo)
+                nc.scalar.activation(y[:, lo : lo + N_COLS], acc, GELU)
 
         def scatter(c, b, y, gate_ap, pieces=1):
             nc.vector.tensor_tensor(windows[b][:].indirect(places[:, entry_cols(c, pieces)]), y, gate_ap, MULT)
@@ -181,11 +197,8 @@ def tile_picked_route2_lingelu_e_kernel(tc, xT, gate, w1_words, w1_scales, offs,
         pass1[0] = quantise("0", PIECE, lead)
         gather_words(3)
         y00 = result_tile("y00")
-        for lo in range(0, PIECE, N_COLS):
-            acc = bank(f"acc_first{lo}", N_COLS)
-            product(acc, 0, 0, lo)
-            nc.scalar.activation(y00[:, lo : lo + N_COLS], acc, GELU)
-        acc01 = multiply(bank("acc01"), 0, 1)
+        first_block(0, y00)
+        acc01 = multiply(bank("acc01", "second"), 0, 1)
         scatter(0, 0, y00, gates[0])
 
         pass1[1] = quantise("1", PIECE, weave(1))
@@ -193,24 +206,23 @@ def tile_picked_route2_lingelu_e_kernel(tc, xT, gate, w1_words, w1_scales, offs,
         nc.scalar.activation(y01, acc01, GELU)
         scatter(0, 1, y01, gates[0])
         y10 = result_tile("y10")
-        nc.scalar.activation(y10, multiply(bank("acc10"), 1, 0), GELU)
-        acc11 = multiply(bank("acc11"), 1, 1)
+        first_block(1, y10)
+        acc11 = multiply(bank("acc11", "second"), 1, 1)
         scatter(1, 0, y10, gates[1])
 
         pass1[2] = quantise("2", PIECE, weave(2))
         y11 = behind_weave(2)
         nc.scalar.activation(y11, acc11, GELU)
         scatter(1, 1, y11, gates[1])
-        acc20 = multiply(bank("acc20"), 2, 0)
-        acc_last = bank("acc_last", 2 * PIECE)
+        acc_last = bank("acc_last", "second", 2 * PIECE)
         multiply(acc_last[:, 0:PIECE], 2, 1)
 
         pass1[3] = quantise("3", PIECE, weave(3))
         y20 = behind_weave(3)
-        nc.scalar.activation(y20, acc20, GELU)
+        first_block(2, y20)
         scatter(2, 0, y20, gates[2])
         y30 = result_tile("y30")
-        nc.scalar.activation(y30, multiply(bank("acc30"), 3, 0), GELU)
+        first_block(3, y30)
         multiply(acc_last[:, PIECE : 2 * PIECE], 3, 1)
         scatter(3, 0, y30, gates[3])
         y_last = behind_weave(3, 2 * PIECE)

@@ -25,16 +25,17 @@ BLOCKS = N // P
 HALF = T // 2
 
 PAIR_LOADS = (
-    ((0, 1024, "vector", 672), (1024, 1024, "vector", 672)),
-    ((0, 1024, "gpsimd", 384), (1024, 1024, "vector", 704)),
-    ((0, 1024, "gpsimd", 384), (1024, 512, "vector", 0), (1536, 512, "vector", 0)),
+    ((0, 2048, "vector", 1344),),
+    ((0, 1280, "gpsimd", 512), (1280, 768, "vector", 448)),
+    ((0, 1280, "gpsimd", 512), (1280, 768, "vector", 192)),
 )
-ROW_SHARES = ((0, 0), (1024, 512))
+ROW_LOADS = (((0, 2048, 960),), ((0, 1024, 896), (1024, 1024, 384)))
 PIECE = 256
 N_COLS = 128
 HALF_PIECE = PIECE // 2
 LOWER = {c: HALF_PIECE + (c - 1) * PIECE for c in (1, 2, 3)}
-UPPER = {c: LOWER[3] + PIECE + (3 - c) * HALF_PIECE for c in (1, 2, 3)}
+UPPER = {c: LOWER[2] + T - (c - 1) * HALF_PIECE for c in (1, 2, 3)}
+LEAD = UPPER[1] + PIECE
 STAGE = 2 * UPPER[1] - LOWER[1]
 
 
@@ -79,7 +80,7 @@ def tile_picked_route2_lingelu_e_kernel(tc, xT, gate, w1_words, w1_scales, offs,
             for first, width, helper, by_helper in loads:
                 raw = keep.tile([P, 2, width], F32, name=f"raw{g}{u}_{first}", align_bytes=64)
                 nc.sync.dma_start(out=raw[:], in_=pair_rows[g, u, :, :, first : first + width])
-                if (g, u, first) == (0, 0, 0):
+                if (g, u) == (0, 0):
                     nc.sync.dma_start(picks[:], offs)
                 for lo, hi, cast in ((0, by_helper, helpers[helper]), (by_helper, width, nc.scalar.copy)):
                     if hi > lo:
@@ -89,15 +90,14 @@ def tile_picked_route2_lingelu_e_kernel(tc, xT, gate, w1_words, w1_scales, offs,
                         )
             return pairs[:].bitcast(U32)
 
-        def load_row(j, shares):
-            raw = keep.tile([P, T], F32, name=f"row{j}", align_bytes=64)
+        def load_row(j, raw, loads):
             rounded = keep.tile([P, T], BF16, name=f"rounded{j}", align_bytes=64)
-            for first, by_gpsimd in zip((0, HALF), shares):
-                nc.sync.dma_start(out=raw[:, first : first + HALF], in_=single_rows[1, j, :, first : first + HALF])
-                for lo, hi, cast in ((0, by_gpsimd, gpsimd_round), (by_gpsimd, HALF, nc.scalar.copy)):
+            for first, width, by_gpsimd in loads:
+                nc.sync.dma_start(out=raw[:, first : first + width], in_=single_rows[1, j, :, first : first + width])
+                for lo, hi, cast in ((0, by_gpsimd, gpsimd_round), (by_gpsimd, width, nc.scalar.copy)):
                     if hi > lo:
                         cast(rounded[:, first + lo : first + hi], raw[:, first + lo : first + hi])
-            return raw, rounded
+            return rounded
 
         def quantise(name, count, woven):
             codes = keep.tile([P, count], U32, name=f"codes{name}", tag=f"codes{name}", align_bytes=64)
@@ -109,28 +109,32 @@ def tile_picked_route2_lingelu_e_kernel(tc, xT, gate, w1_words, w1_scales, offs,
             )
             return codes, scales
 
-        woven0 = keep.tile([P, S, 2], U32, name="woven0", align_bytes=64)
+        woven0 = [keep.tile([P, S // 2, 2], U32, name=f"woven0_{h}", align_bytes=64) for h in range(2)]
         for u in range(2):
             words = load_pair(0, u, PAIR_LOADS[u])
-            nc.vector.tensor_copy(woven0[:, :, u], words.indirect(picks[:]))
-        pass0 = quantise("_pass0", S, woven0[:].rearrange("p s u -> p (s u)"))
+            for h in range(2):
+                nc.vector.tensor_copy(woven0[h][:, :, u], words.indirect(picks[:, entry_cols(2 * h, 2)]))
+        pass0 = [quantise(f"_pass0_{h}", S // 2, woven0[h][:].rearrange("p s u -> p (s u)")) for h in range(2)]
         pass1 = {}
 
         words = load_pair(1, 0, PAIR_LOADS[2])
         stage = keep.tile([P, STAGE], U32, name="stage", align_bytes=64)
-        lead = stage[:, LOWER[3] : LOWER[3] + 2 * PIECE]
+        lead = stage[:, LEAD : LEAD + 2 * PIECE]
         lead_rows = lead.bitcast(BF16).rearrange("p (s j) -> p s j", j=4)
         lead_picks = picks[:, entry_cols(0)]
         nc.vector.tensor_copy(lead.rearrange("p (s u) -> p s u", u=2)[:, :, 0], words.indirect(lead_picks))
 
-        def gather_words(c):
-            nc.vector.tensor_copy(stage[:, LOWER[c] : LOWER[c] + PIECE], words.indirect(picks[:, entry_cols(c)]))
+        def gather_words(c, pieces):
+            nc.vector.tensor_copy(
+                stage[:, LOWER[c] : LOWER[c] + pieces * PIECE], words.indirect(picks[:, entry_cols(c, pieces)])
+            )
 
-        gather_words(1)
-        gather_words(2)
-        raw2, rounded2 = load_row(2, ROW_SHARES[0])
-        nc.vector.tensor_copy(lead_rows[:, :, 2], raw2[:].indirect(lead_picks))
-        raw3, rounded3 = load_row(3, ROW_SHARES[1])
+        gather_words(1, 1)
+        row2 = keep.tile([P, T], F32, name="row2", align_bytes=64)
+        rounded2 = load_row(2, row2[:], ROW_LOADS[0])
+        nc.vector.tensor_copy(lead_rows[:, :, 2], row2[:].indirect(lead_picks))
+        row3 = stage[:, LOWER[2] : LOWER[2] + T].bitcast(F32)
+        rounded3 = load_row(3, row3, ROW_LOADS[1])
 
         w_words = keep.tile([P, PASSES, 2 * N], U8, name="w_words", align_bytes=64)
         nc.sync.dma_start(out=w_words[:].bitcast(I32), in_=w1_words.bitcast(I32).rearrange("g p n -> p g n"))
@@ -159,7 +163,7 @@ def tile_picked_route2_lingelu_e_kernel(tc, xT, gate, w1_words, w1_scales, offs,
             return stage[:, first : first + width].bitcast(F32)
 
         def product(acc, c, b, lo):
-            for g, (codes, scales), start in ((0, pass0, c * PIECE + lo), (1, pass1[c], lo)):
+            for g, (codes, scales), start in ((0, pass0[c // 2], c % 2 * PIECE + lo), (1, pass1[c], lo)):
                 entries = slice(start, start + N_COLS)
                 nc.tensor.matmul_mx(
                     out=acc,
@@ -193,9 +197,9 @@ def tile_picked_route2_lingelu_e_kernel(tc, xT, gate, w1_words, w1_scales, offs,
             y = keep.tile([P, PIECE], F32, name=name)
             return y[:]
 
-        nc.vector.tensor_copy(lead_rows[:, :, 3], raw3[:].indirect(lead_picks))
+        nc.vector.tensor_copy(lead_rows[:, :, 3], row3.indirect(lead_picks))
         pass1[0] = quantise("0", PIECE, lead)
-        gather_words(3)
+        gather_words(2, 2)
         y00 = result_tile("y00")
         first_block(0, y00)
         acc01 = multiply(bank("acc01", "second"), 0, 1)

@@ -26,8 +26,8 @@ HALF = T // 2
 
 PAIR_LOADS = (
     ((0, 2048, "vector", 1344),),
-    ((0, 1280, "gpsimd", 512), (1280, 768, "vector", 448)),
-    ((0, 1280, "gpsimd", 512), (1280, 768, "vector", 192)),
+    ((0, 1024, "gpsimd", 448), (1024, 2048, "vector", 640)),
+    ((0, 1024, "gpsimd", 448), (1024, 2048, "vector", 384)),
 )
 ROW_LOADS = (((0, 2048, 960),), ((0, 1024, 896), (1024, 1024, 384)))
 PIECE = 256
@@ -64,7 +64,7 @@ def tile_picked_route2_lingelu_e_kernel(tc, xT, gate, w1_words, w1_scales, offs,
                 in_=w1_scales.bitcast(I32)[:, 4 * q : 4 * q + 4, :].rearrange("g r n -> r g n"),
             )
 
-        pair_rows = xT.rearrange("(g p u e) t -> g u p e t", g=PASSES, p=P, u=2, e=2)
+        pair_rows = xT.rearrange("(g p u e) t -> g u p (e t)", g=PASSES, p=P, u=2, e=2)
         single_rows = xT.rearrange("(g p j) t -> g j p t", g=PASSES, p=P, j=4)
 
         def entry_cols(c, pieces=1):
@@ -77,17 +77,19 @@ def tile_picked_route2_lingelu_e_kernel(tc, xT, gate, w1_words, w1_scales, offs,
 
         def load_pair(g, u, loads):
             pairs = keep.tile([P, 2 * T], BF16, name=f"pairs{g}{u}", align_bytes=64)
-            for first, width, helper, by_helper in loads:
-                raw = keep.tile([P, 2, width], F32, name=f"raw{g}{u}_{first}", align_bytes=64)
-                nc.sync.dma_start(out=raw[:], in_=pair_rows[g, u, :, :, first : first + width])
+            raw = keep.tile([P, 2 * T], F32, name=f"raw{g}{u}", align_bytes=64)
+            both = raw[:].rearrange("p (e t) -> p e t", e=2)
+            for first, end, helper, by_helper in loads:
+                run = slice(T + first if first else 0, T + end)
+                nc.sync.dma_start(out=raw[:, run], in_=pair_rows[g, u, :, run])
                 if (g, u) == (0, 0):
                     nc.sync.dma_start(picks[:], offs)
-                for lo, hi, cast in ((0, by_helper, helpers[helper]), (by_helper, width, nc.scalar.copy)):
-                    if hi > lo:
-                        cast(
-                            pairs[:, 2 * (first + lo) : 2 * (first + hi)].rearrange("p (c i e) -> p c e i", i=4, e=2),
-                            raw[:, :, lo:hi].rearrange("p e (c i) -> p c e i", i=4),
-                        )
+                split = first + by_helper
+                for lo, hi, cast in ((first, split, helpers[helper]), (split, end, nc.scalar.copy)):
+                    cast(
+                        pairs[:, 2 * lo : 2 * hi].rearrange("p (c i e) -> p c e i", i=4, e=2),
+                        both[:, :, lo:hi].rearrange("p e (c i) -> p c e i", i=4),
+                    )
             return pairs[:].bitcast(U32)
 
         def load_row(j, raw, loads):

@@ -26,8 +26,8 @@ HALF = T // 2
 
 PAIR_LOADS = (
     ((0, 2048, "vector", 1344),),
-    ((0, 1024, "gpsimd", 448), (1024, 2048, "vector", 640)),
-    ((0, 1024, "gpsimd", 448), (1024, 2048, "vector", 384)),
+    ((0, 1024, "gpsimd", 416), (1024, 2048, "vector", 672)),
+    ((0, 1024, "gpsimd", 192), (1024, 2048, "vector", 704)),
 )
 ROW_LOADS = (((0, 2048, 960),), ((0, 1024, 896), (1024, 1024, 384)))
 PIECE = 256
@@ -82,7 +82,7 @@ def tile_picked_route2_lingelu_e_kernel(tc, xT, gate, w1_words, w1_scales, offs,
             for first, end, helper, by_helper in loads:
                 run = slice(T + first if first else 0, T + end)
                 nc.sync.dma_start(out=raw[:, run], in_=pair_rows[g, u, :, run])
-                if (g, u) == (0, 0):
+                if (g, u, first) == (0, 0, 0):
                     nc.sync.dma_start(picks[:], offs)
                 split = first + by_helper
                 for lo, hi, cast in ((first, split, helpers[helper]), (split, end, nc.scalar.copy)):
@@ -104,19 +104,21 @@ def tile_picked_route2_lingelu_e_kernel(tc, xT, gate, w1_words, w1_scales, offs,
         def quantise(name, count, woven):
             codes = keep.tile([P, count], U32, name=f"codes{name}", tag=f"codes{name}", align_bytes=64)
             scales = keep.tile([P, count], U8, name=f"scales{name}", align_bytes=64)
-            nc.vector.quantize_mx(
-                out=codes[:].bitcast(FP8X4),
-                scales=scales[:],
-                in_=woven.bitcast(BF16),
-            )
-            return codes, scales
+            nc.vector.quantize_mx(out=codes[:].bitcast(FP8X4), scales=scales[:], in_=woven.bitcast(BF16))
+            return [(codes[:, lo : lo + N_COLS], scales[:, lo : lo + N_COLS]) for lo in range(0, count, N_COLS)]
 
         woven0 = [keep.tile([P, S // 2, 2], U32, name=f"woven0_{h}", align_bytes=64) for h in range(2)]
+        halves0 = keep.tile([P, 2, S // 2], U32, name="halves0", align_bytes=64)
         for u in range(2):
             words = load_pair(0, u, PAIR_LOADS[u])
-            for h in range(2):
-                nc.vector.tensor_copy(woven0[h][:, :, u], words.indirect(picks[:, entry_cols(2 * h, 2)]))
-        pass0 = [quantise(f"_pass0_{h}", S // 2, woven0[h][:].rearrange("p s u -> p (s u)")) for h in range(2)]
+            nc.vector.tensor_copy(halves0[:, u, :], words.indirect(picks[:, entry_cols(2, 2)]))
+            nc.vector.tensor_copy(woven0[0][:, :, u], words.indirect(picks[:, entry_cols(0, 2)]))
+        nc.scalar.copy(
+            woven0[1][:].rearrange("p (c i) u -> p c u i", i=4),
+            halves0[:].rearrange("p u (c i) -> p c u i", i=4),
+        )
+        second = quantise("_pass0_1", S // 2, woven0[1][:].rearrange("p s u -> p (s u)"))
+        pass0 = quantise("_pass0_0", S // 2, woven0[0][:].rearrange("p s u -> p (s u)")) + second
         pass1 = {}
 
         words = load_pair(1, 0, PAIR_LOADS[2])
@@ -165,14 +167,13 @@ def tile_picked_route2_lingelu_e_kernel(tc, xT, gate, w1_words, w1_scales, offs,
             return stage[:, first : first + width].bitcast(F32)
 
         def product(acc, c, b, lo):
-            for g, (codes, scales), start in ((0, pass0[c // 2], c % 2 * PIECE + lo), (1, pass1[c], lo)):
-                entries = slice(start, start + N_COLS)
+            for g, (codes, scales) in enumerate((pass0[(c * PIECE + lo) // N_COLS], pass1[c][lo // N_COLS])):
                 nc.tensor.matmul_mx(
                     out=acc,
                     lhsT=w_words[:, g, 2 * P * b : 2 * P * (b + 1)].bitcast(FP4X4),
                     lhsT_scale=w_scales[:, g, P * b : P * (b + 1)],
-                    rhs=codes[:, entries].bitcast(FP8X4),
-                    rhs_scale=scales[:, entries],
+                    rhs=codes.bitcast(FP8X4),
+                    rhs_scale=scales,
                     start=(g == 0),
                     stop=(g == PASSES - 1),
                 )

@@ -20,22 +20,26 @@ ADD = mybir.AluOpType.add
 
 P = 128
 PASSES = K // 512
-PER_COL = 16
 BLOCKS = N // P
-HALF = T // 2
+PER_COL = 16
+N_COLS = 128
+WALK = 4
 
-PAIR_LOADS = (
+PAIR_STEPS = (
     ((0, 2048, "vector", 1344),),
     ((0, 1024, "gpsimd", 416), (1024, 2048, "vector", 672)),
     ((0, 1024, "gpsimd", 192), (1024, 2048, "vector", 704)),
 )
-ROW_LOADS = (((0, 2048, 960),), ((0, 1024, 896), (1024, 1024, 384)))
-PIECE = 256
-N_COLS = 128
-HALF_PIECE = PIECE // 2
-LOWER = {c: HALF_PIECE + (c - 1) * PIECE for c in (1, 2, 3)}
-UPPER = {c: LOWER[2] + T - (c - 1) * HALF_PIECE for c in (1, 2, 3)}
-LEAD = UPPER[1] + PIECE
+ROW_LOADS = {2: ((0, 2048, 960),), 3: ((0, 1024, 1024), (1024, 1024, 448))}
+
+LEAD_COUNT = 256
+COUNT = (S - LEAD_COUNT) // 2
+PIECES = ((0, LEAD_COUNT), (LEAD_COUNT, COUNT), (LEAD_COUNT + COUNT, COUNT))
+PARTS = (COUNT - N_COLS, N_COLS)
+
+LOWER = {1: LEAD_COUNT - N_COLS, 2: LEAD_COUNT - N_COLS + COUNT}
+UPPER = {1: LOWER[2] + T, 2: LOWER[2] + T + N_COLS - COUNT}
+LEAD = UPPER[1] + COUNT
 STAGE = 2 * UPPER[1] - LOWER[1]
 
 
@@ -67,107 +71,112 @@ def tile_picked_route2_lingelu_e_kernel(tc, xT, gate, w1_words, w1_scales, offs,
         pair_rows = xT.rearrange("(g p u e) t -> g u p (e t)", g=PASSES, p=P, u=2, e=2)
         single_rows = xT.rearrange("(g p j) t -> g j p t", g=PASSES, p=P, j=4)
 
-        def entry_cols(c, pieces=1):
-            return slice(c * PIECE // PER_COL, (c + pieces) * PIECE // PER_COL)
+        def entry_cols(first, count):
+            return slice(first // PER_COL, (first + count) // PER_COL)
 
         def gpsimd_round(target, source):
             nc.gpsimd.tensor_scalar(target, source, 1.0, 0.0, MULT, ADD)
 
         helpers = {"vector": nc.vector.tensor_copy, "gpsimd": gpsimd_round}
 
-        def load_pair(g, u, loads):
+        def load_pair(g, u, steps):
             pairs = keep.tile([P, 2 * T], BF16, name=f"pairs{g}{u}", align_bytes=64)
             raw = keep.tile([P, 2 * T], F32, name=f"raw{g}{u}", align_bytes=64)
             both = raw[:].rearrange("p (e t) -> p e t", e=2)
-            for first, end, helper, by_helper in loads:
+            for first, end, helper, by_helper in steps:
                 run = slice(T + first if first else 0, T + end)
                 nc.sync.dma_start(out=raw[:, run], in_=pair_rows[g, u, :, run])
-                if (g, u, first) == (0, 0, 0):
+                if (g, u) == (0, 0):
                     nc.sync.dma_start(picks[:], offs)
                 split = first + by_helper
                 for lo, hi, cast in ((first, split, helpers[helper]), (split, end, nc.scalar.copy)):
                     cast(
-                        pairs[:, 2 * lo : 2 * hi].rearrange("p (c i e) -> p c e i", i=4, e=2),
-                        both[:, :, lo:hi].rearrange("p e (c i) -> p c e i", i=4),
+                        pairs[:, 2 * lo : 2 * hi].rearrange("p (c i e) -> p c e i", i=WALK, e=2),
+                        both[:, :, lo:hi].rearrange("p e (c i) -> p c e i", i=WALK),
                     )
             return pairs[:].bitcast(U32)
 
-        def load_row(j, raw, loads):
+        def load_row(j, raw):
             rounded = keep.tile([P, T], BF16, name=f"rounded{j}", align_bytes=64)
-            for first, width, by_gpsimd in loads:
-                nc.sync.dma_start(out=raw[:, first : first + width], in_=single_rows[1, j, :, first : first + width])
-                for lo, hi, cast in ((0, by_gpsimd, gpsimd_round), (by_gpsimd, width, nc.scalar.copy)):
-                    if hi > lo:
-                        cast(rounded[:, first + lo : first + hi], raw[:, first + lo : first + hi])
+            for first, width, by_gpsimd in ROW_LOADS[j]:
+                end, split = first + width, first + by_gpsimd
+                nc.sync.dma_start(out=raw[:, first:end], in_=single_rows[1, j, :, first:end])
+                gpsimd_round(rounded[:, first:split], raw[:, first:split])
+                if split < end:
+                    nc.scalar.copy(rounded[:, split:end], raw[:, split:end])
             return rounded
 
-        def quantise(name, count, woven):
-            codes = keep.tile([P, count], U32, name=f"codes{name}", tag=f"codes{name}", align_bytes=64)
-            scales = keep.tile([P, count], U8, name=f"scales{name}", align_bytes=64)
-            nc.vector.quantize_mx(out=codes[:].bitcast(FP8X4), scales=scales[:], in_=woven.bitcast(BF16))
-            return [(codes[:, lo : lo + N_COLS], scales[:, lo : lo + N_COLS]) for lo in range(0, count, N_COLS)]
+        def quantise(name, woven, widths):
+            codes = keep.tile([P, sum(widths)], U32, name=f"codes{name}", tag=f"codes{name}", align_bytes=64)
+            scales = keep.tile([P, sum(widths)], U8, name=f"scales{name}", align_bytes=64)
+            lo = 0
+            for width in widths:
+                nc.vector.quantize_mx(
+                    out=codes[:, lo : lo + width].bitcast(FP8X4),
+                    scales=scales[:, lo : lo + width],
+                    in_=woven[:, 2 * lo : 2 * (lo + width)].bitcast(BF16),
+                )
+                lo = lo + width
+            return [(codes[:, n : n + N_COLS], scales[:, n : n + N_COLS]) for n in range(0, lo, N_COLS)]
 
         woven0 = [keep.tile([P, S // 2, 2], U32, name=f"woven0_{h}", align_bytes=64) for h in range(2)]
         halves0 = keep.tile([P, 2, S // 2], U32, name="halves0", align_bytes=64)
         for u in range(2):
-            words = load_pair(0, u, PAIR_LOADS[u])
-            nc.vector.tensor_copy(halves0[:, u, :], words.indirect(picks[:, entry_cols(2, 2)]))
-            nc.vector.tensor_copy(woven0[0][:, :, u], words.indirect(picks[:, entry_cols(0, 2)]))
+            words0 = load_pair(0, u, PAIR_STEPS[u])
+            nc.vector.tensor_copy(halves0[:, u, :], words0.indirect(picks[:, entry_cols(S // 2, S // 2)]))
+            nc.vector.tensor_copy(woven0[0][:, :, u], words0.indirect(picks[:, entry_cols(0, S // 2)]))
         nc.scalar.copy(
-            woven0[1][:].rearrange("p (c i) u -> p c u i", i=4),
-            halves0[:].rearrange("p u (c i) -> p c u i", i=4),
+            woven0[1][:].rearrange("p (c i) u -> p c u i", i=WALK),
+            halves0[:].rearrange("p u (c i) -> p c u i", i=WALK),
         )
-        second = quantise("_pass0_1", S // 2, woven0[1][:].rearrange("p s u -> p (s u)"))
-        pass0 = quantise("_pass0_0", S // 2, woven0[0][:].rearrange("p s u -> p (s u)")) + second
-        pass1 = {}
+        second_half = quantise("_pass0_1", woven0[1][:].rearrange("p s u -> p (s u)"), (S // 2,))
+        pass0 = quantise("_pass0_0", woven0[0][:].rearrange("p s u -> p (s u)"), (S // 2,)) + second_half
 
-        words = load_pair(1, 0, PAIR_LOADS[2])
+        words1 = load_pair(1, 0, PAIR_STEPS[2])
         stage = keep.tile([P, STAGE], U32, name="stage", align_bytes=64)
-        lead = stage[:, LEAD : LEAD + 2 * PIECE]
+        lead = stage[:, LEAD : LEAD + 2 * LEAD_COUNT]
         lead_rows = lead.bitcast(BF16).rearrange("p (s j) -> p s j", j=4)
-        lead_picks = picks[:, entry_cols(0)]
-        nc.vector.tensor_copy(lead.rearrange("p (s u) -> p s u", u=2)[:, :, 0], words.indirect(lead_picks))
+        lead_picks = picks[:, entry_cols(*PIECES[0])]
+        nc.vector.tensor_copy(lead.rearrange("p (s u) -> p s u", u=2)[:, :, 0], words1.indirect(lead_picks))
 
-        def gather_words(c, pieces):
-            nc.vector.tensor_copy(
-                stage[:, LOWER[c] : LOWER[c] + pieces * PIECE], words.indirect(picks[:, entry_cols(c, pieces)])
-            )
+        def gather_lower(c):
+            nc.vector.tensor_copy(stage[:, LOWER[c] : LOWER[c] + COUNT], words1.indirect(picks[:, entry_cols(*PIECES[c])]))
 
-        gather_words(1, 1)
+        def gather_upper(c, e, rounded):
+            upper = stage[:, UPPER[c] : UPPER[c] + COUNT].bitcast(BF16).rearrange("p (s e) -> p s e", e=2)
+            nc.scalar.activation(upper[:, :, e], rounded[:].indirect(picks[:, entry_cols(*PIECES[c])]), COPY)
+
+        gather_lower(1)
         row2 = keep.tile([P, T], F32, name="row2", align_bytes=64)
-        rounded2 = load_row(2, row2[:], ROW_LOADS[0])
+        rounded2 = load_row(2, row2[:])
         nc.vector.tensor_copy(lead_rows[:, :, 2], row2[:].indirect(lead_picks))
+        gather_upper(1, 0, rounded2)
         row3 = stage[:, LOWER[2] : LOWER[2] + T].bitcast(F32)
-        rounded3 = load_row(3, row3, ROW_LOADS[1])
+        rounded3 = load_row(3, row3)
 
         w_words = keep.tile([P, PASSES, 2 * N], U8, name="w_words", align_bytes=64)
         nc.sync.dma_start(out=w_words[:].bitcast(I32), in_=w1_words.bitcast(I32).rearrange("g p n -> p g n"))
         nc.sync.dma_start(places[:], dst)
-        gate_tiles = []
-        for first, count in ((0, PIECE), (PIECE, PIECE), (2 * PIECE, 2 * PIECE)):
+        gates = []
+        for first, count in PIECES:
             gate_sb = keep.tile([P, count], F32, name=f"gate{first}")
             nc.sync.dma_start(out=gate_sb[:], in_=gate[:, first : first + count])
-            gate_tiles.append(gate_sb)
-        gates = [gate_tiles[0][:], gate_tiles[1][:], gate_tiles[2][:, 0:PIECE], gate_tiles[2][:, PIECE : 2 * PIECE]]
+            gates.append(gate_sb[:])
 
-        def weave(c):
-            upper = stage[:, UPPER[c] : UPPER[c] + PIECE].bitcast(BF16).rearrange("p (s e) -> p s e", e=2)
-            for e, rounded in enumerate((rounded2, rounded3)):
-                nc.scalar.activation(upper[:, :, e], rounded[:].indirect(picks[:, entry_cols(c)]), COPY)
+        def weave(c, tag):
             both = stage[:, LOWER[c] : 2 * UPPER[c] - LOWER[c]].rearrange("p (u r) -> p u r", u=2)
-            source = both[:, :, 0:PIECE].rearrange("p u (h c i) -> p h c u i", h=2, i=4)
-            woven = keep.tile([P, 2 * PIECE], U32, name=f"woven1_{c}", tag="codes0" if c == 1 else f"woven{c}", align_bytes=64)
-            target = woven[:].rearrange("p (h c i u) -> p h c u i", h=2, i=4, u=2)
-            for h in range(2):
-                nc.scalar.copy(target[:, h], source[:, h])
+            woven = keep.tile([P, 2 * COUNT], U32, name=f"woven1_{c}", tag=tag, align_bytes=64)
+            for lo, hi in ((0, PARTS[0]), (PARTS[0], COUNT)):
+                nc.scalar.copy(
+                    woven[:, 2 * lo : 2 * hi].rearrange("p (c i u) -> p c u i", i=WALK, u=2),
+                    both[:, :, lo:hi].rearrange("p u (c i) -> p c u i", i=WALK),
+                )
             return woven[:]
 
-        def behind_weave(c, width=PIECE):
-            first = LOWER[c] - HALF_PIECE
-            return stage[:, first : first + width].bitcast(F32)
+        pass1 = {}
 
         def product(acc, c, b, lo):
-            for g, (codes, scales) in enumerate((pass0[(c * PIECE + lo) // N_COLS], pass1[c][lo // N_COLS])):
+            for g, (codes, scales) in enumerate((pass0[(PIECES[c][0] + lo) // N_COLS], pass1[c][lo // N_COLS])):
                 nc.tensor.matmul_mx(
                     out=acc,
                     lhsT=w_words[:, g, 2 * P * b : 2 * P * (b + 1)].bitcast(FP4X4),
@@ -178,63 +187,48 @@ def tile_picked_route2_lingelu_e_kernel(tc, xT, gate, w1_words, w1_scales, offs,
                     stop=(g == PASSES - 1),
                 )
 
-        def multiply(acc, c, b):
-            for lo in range(0, PIECE, N_COLS):
-                product(acc[:, lo : lo + N_COLS], c, b, lo)
-            return acc
-
-        def bank(name, tag, width=PIECE):
-            acc = psum.tile([P, width], F32, name=name, tag=tag)
-            return acc[:]
-
-        def first_block(c, y):
-            for lo in range(0, PIECE, N_COLS):
-                acc = bank(f"acc{c}_{lo}", f"first{lo}", N_COLS)
-                product(acc, c, 0, lo)
-                nc.scalar.activation(y[:, lo : lo + N_COLS], acc, GELU)
-
-        def scatter(c, b, y, gate_ap, pieces=1):
-            nc.vector.tensor_tensor(windows[b][:].indirect(places[:, entry_cols(c, pieces)]), y, gate_ap, MULT)
-
-        def result_tile(name):
-            y = keep.tile([P, PIECE], F32, name=name)
+        def block0_results(c):
+            count = PIECES[c][1]
+            y = keep.tile([P, count], F32, name=f"y{c}_0")
+            for lo in range(0, count, N_COLS):
+                acc = psum.tile([P, N_COLS], F32, name=f"acc{c}_{lo}", tag=f"first{lo}")
+                product(acc[:], c, 0, lo)
+                nc.scalar.activation(y[:, lo : lo + N_COLS], acc[:], GELU)
             return y[:]
 
+        def block1_sums(c):
+            count = PIECES[c][1]
+            acc = psum.tile([P, count], F32, name=f"acc{c}_second", tag="second")
+            for lo in range(0, count, N_COLS):
+                product(acc[:, lo : lo + N_COLS], c, 1, lo)
+            return acc[:]
+
+        def scatter(c, b, y):
+            nc.vector.tensor_tensor(windows[b][:].indirect(places[:, entry_cols(*PIECES[c])]), y, gates[c], MULT)
+
         nc.vector.tensor_copy(lead_rows[:, :, 3], row3.indirect(lead_picks))
-        pass1[0] = quantise("0", PIECE, lead)
-        gather_words(2, 2)
-        y00 = result_tile("y00")
-        first_block(0, y00)
-        acc01 = multiply(bank("acc01", "second"), 0, 1)
-        scatter(0, 0, y00, gates[0])
+        pass1[0] = quantise("0", lead, (LEAD_COUNT,))
+        gather_lower(2)
 
-        pass1[1] = quantise("1", PIECE, weave(1))
-        y01 = behind_weave(1)
-        nc.scalar.activation(y01, acc01, GELU)
-        scatter(0, 1, y01, gates[0])
-        y10 = result_tile("y10")
-        first_block(1, y10)
-        acc11 = multiply(bank("acc11", "second"), 1, 1)
-        scatter(1, 0, y10, gates[1])
-
-        pass1[2] = quantise("2", PIECE, weave(2))
-        y11 = behind_weave(2)
-        nc.scalar.activation(y11, acc11, GELU)
-        scatter(1, 1, y11, gates[1])
-        acc_last = bank("acc_last", "second", 2 * PIECE)
-        multiply(acc_last[:, 0:PIECE], 2, 1)
-
-        pass1[3] = quantise("3", PIECE, weave(3))
-        y20 = behind_weave(3)
-        first_block(2, y20)
-        scatter(2, 0, y20, gates[2])
-        y30 = result_tile("y30")
-        first_block(3, y30)
-        multiply(acc_last[:, PIECE : 2 * PIECE], 3, 1)
-        scatter(3, 0, y30, gates[3])
-        y_last = behind_weave(3, 2 * PIECE)
-        nc.scalar.activation(y_last, acc_last, GELU)
-        scatter(2, 1, y_last, gate_tiles[2][:], 2)
+        for c, (first, count) in enumerate(PIECES):
+            y0 = block0_results(c)
+            sums1 = block1_sums(c)
+            scatter(c, 0, y0)
+            if c + 1 < len(PIECES):
+                if c == 0:
+                    tag = "codes0"
+                else:
+                    tag = "woven2"
+                    gather_upper(c + 1, 0, rounded2)
+                gather_upper(c + 1, 1, rounded3)
+                pass1[c + 1] = quantise(f"{c + 1}", weave(c + 1, tag), PARTS)
+                end = LOWER[c + 1] + N_COLS
+                y1 = stage[:, end - count : end].bitcast(F32)
+            else:
+                y_last = keep.tile([P, count], F32, name="y_last")
+                y1 = y_last[:]
+            nc.scalar.activation(y1, sums1, GELU)
+            scatter(c, 1, y1)
 
         for b in range(BLOCKS):
             nc.sync.dma_start(out=out[P * b : P * (b + 1), :], in_=windows[b][:])

@@ -28,7 +28,7 @@ WALK = 4
 PAIR_STEPS = (
     ((0, 2048, "vector", 1344),),
     ((0, 1024, "gpsimd", 416), (1024, 2048, "vector", 672)),
-    ((0, 1024, "gpsimd", 192), (1024, 2048, "vector", 704)),
+    ((0, 1024, "gpsimd", 192), (1024, 2048, "vector", 608)),
 )
 ROW_LOADS = {2: ((0, 2048, 960),), 3: ((0, 1024, 1024), (1024, 1024, 448))}
 
@@ -38,7 +38,9 @@ PIECES = ((0, LEAD_COUNT), (LEAD_COUNT, COUNT), (LEAD_COUNT + COUNT, COUNT))
 PARTS = (COUNT - N_COLS, N_COLS)
 
 LOWER = {1: LEAD_COUNT - N_COLS, 2: LEAD_COUNT - N_COLS + COUNT}
-UPPER = {1: LOWER[2] + T, 2: LOWER[2] + T + N_COLS - COUNT}
+LATE = 512
+ROW3 = LOWER[2] + COUNT - LATE
+UPPER = {1: ROW3 + T, 2: ROW3 + T + N_COLS - COUNT}
 LEAD = UPPER[1] + COUNT
 STAGE = 2 * UPPER[1] - LOWER[1]
 
@@ -139,19 +141,20 @@ def tile_picked_route2_lingelu_e_kernel(tc, xT, gate, w1_words, w1_scales, offs,
         lead_picks = picks[:, entry_cols(*PIECES[0])]
         nc.vector.tensor_copy(lead.rearrange("p (s u) -> p s u", u=2)[:, :, 0], words1.indirect(lead_picks))
 
-        def gather_lower(c):
-            nc.vector.tensor_copy(stage[:, LOWER[c] : LOWER[c] + COUNT], words1.indirect(picks[:, entry_cols(*PIECES[c])]))
+        def gather_lower(first, count):
+            at = LOWER[1] + first - LEAD_COUNT
+            nc.vector.tensor_copy(stage[:, at : at + count], words1.indirect(picks[:, entry_cols(first, count)]))
 
         def gather_upper(c, e, rounded):
             upper = stage[:, UPPER[c] : UPPER[c] + COUNT].bitcast(BF16).rearrange("p (s e) -> p s e", e=2)
             nc.scalar.activation(upper[:, :, e], rounded[:].indirect(picks[:, entry_cols(*PIECES[c])]), COPY)
 
-        gather_lower(1)
+        gather_lower(LEAD_COUNT, S - LEAD_COUNT - LATE)
         row2 = keep.tile([P, T], F32, name="row2", align_bytes=64)
         rounded2 = load_row(2, row2[:])
         nc.vector.tensor_copy(lead_rows[:, :, 2], row2[:].indirect(lead_picks))
         gather_upper(1, 0, rounded2)
-        row3 = stage[:, LOWER[2] : LOWER[2] + T].bitcast(F32)
+        row3 = stage[:, ROW3 : ROW3 + T].bitcast(F32)
         rounded3 = load_row(3, row3)
 
         w_words = keep.tile([P, PASSES, 2 * N], U8, name="w_words", align_bytes=64)
@@ -208,7 +211,7 @@ def tile_picked_route2_lingelu_e_kernel(tc, xT, gate, w1_words, w1_scales, offs,
 
         nc.vector.tensor_copy(lead_rows[:, :, 3], row3.indirect(lead_picks))
         pass1[0] = quantise("0", lead, (LEAD_COUNT,))
-        gather_lower(2)
+        gather_lower(S - LATE, LATE)
 
         for c, (first, count) in enumerate(PIECES):
             y0 = block0_results(c)

@@ -28,9 +28,9 @@ WALK = 4
 PAIR_STEPS = (
     ((0, 2048, "vector", 1344),),
     ((0, 1024, "gpsimd", 416), (1024, 2048, "vector", 672)),
-    ((0, 1024, "gpsimd", 192), (1024, 2048, "vector", 608)),
+    ((0, 1024, "gpsimd", 192), (1024, 2048, "vector", 672)),
 )
-ROW_LOADS = {2: ((0, 2048, 960),), 3: ((0, 1024, 1024), (1024, 1024, 448))}
+ROW_LOADS = {2: ((0, 2048, 1024),), 3: ((0, 1024, 1024), (1024, 1024, 432))}
 
 LEAD_COUNT = 256
 COUNT = (S - LEAD_COUNT) // 2

@@ -16,39 +16,25 @@ FP4X4 = mybir.dt.float4_e2m1fn_x4
 GELU = mybir.ActivationFunctionType.Gelu_apprx_tanh
 COPY = mybir.ActivationFunctionType.Copy
 MULT = mybir.AluOpType.mult
-ADD = mybir.AluOpType.add
 
 P = 128
 PASSES = K // 512
+PACK = 4
 BLOCKS = N // P
 PER_COL = 16
-N_COLS = 128
 WALK = 4
+DIRECT0 = S // 2
 
-PAIR_STEPS = (
-    ((0, 2048, "vector", 1344),),
-    ((0, 1024, "gpsimd", 416), (1024, 2048, "vector", 672)),
-    ((0, 1024, "gpsimd", 192), (1024, 2048, "vector", 672)),
-)
-ROW_LOADS = {2: ((0, 2048, 1024),), 3: ((0, 1024, 1024), (1024, 1024, 432))}
-
-LEAD_COUNT = 256
-COUNT = (S - LEAD_COUNT) // 2
-PIECES = ((0, LEAD_COUNT), (LEAD_COUNT, COUNT), (LEAD_COUNT + COUNT, COUNT))
-PARTS = (COUNT - N_COLS, N_COLS)
-
-LOWER = {1: LEAD_COUNT - N_COLS, 2: LEAD_COUNT - N_COLS + COUNT}
-LATE = 512
-ROW3 = LOWER[2] + COUNT - LATE
-UPPER = {1: ROW3 + T, 2: ROW3 + T + N_COLS - COUNT}
-LEAD = UPPER[1] + COUNT
-STAGE = 2 * UPPER[1] - LOWER[1]
+LEAD = 256
+COUNT = (S - LEAD) // 2
+A, B, C = (0, LEAD), (LEAD, COUNT), (LEAD + COUNT, COUNT)
 
 
 def tile_picked_route2_lingelu_e_kernel(tc, xT, gate, w1_words, w1_scales, offs, dst, out):
     nc = tc.nc
     with ExitStack() as ctx:
         keep = ctx.enter_context(tc.tile_pool(name="keep", bufs=1))
+        tail = ctx.enter_context(tc.tile_pool(name="tail", bufs=1))
         psum = ctx.enter_context(tc.psum_pool(name="psum", bufs=1))
 
         picks = keep.tile([P, S // PER_COL], U16, name="picks")
@@ -70,168 +56,134 @@ def tile_picked_route2_lingelu_e_kernel(tc, xT, gate, w1_words, w1_scales, offs,
                 in_=w1_scales.bitcast(I32)[:, 4 * q : 4 * q + 4, :].rearrange("g r n -> r g n"),
             )
 
-        pair_rows = xT.rearrange("(g p u e) t -> g u p (e t)", g=PASSES, p=P, u=2, e=2)
-        single_rows = xT.rearrange("(g p j) t -> g j p t", g=PASSES, p=P, j=4)
+        rows = xT.rearrange("(g p j) t -> g j p t", g=PASSES, p=P, j=PACK)
 
-        def entry_cols(first, count):
+        def cols(first, count):
             return slice(first // PER_COL, (first + count) // PER_COL)
 
-        def gpsimd_round(target, source):
-            nc.gpsimd.tensor_scalar(target, source, 1.0, 0.0, MULT, ADD)
+        def load_row(g, j):
+            row = keep.tile([P, T], F32, name=f"row{g}{j}", align_bytes=64)
+            nc.sync.dma_start(out=row[:], in_=rows[g, j])
+            if (g, j) == (0, 0):
+                nc.sync.dma_start(picks[:], offs)
+            return row
 
-        helpers = {"vector": nc.vector.tensor_copy, "gpsimd": gpsimd_round}
+        def gather_woven(woven, j, row, first, count):
+            slot = woven.rearrange("p (s j) -> p s j", j=PACK)[:, :, j]
+            nc.vector.tensor_copy(slot, row[:].indirect(picks[:, cols(first, count)]))
 
-        def load_pair(g, u, steps):
-            pairs = keep.tile([P, 2 * T], BF16, name=f"pairs{g}{u}", align_bytes=64)
-            raw = keep.tile([P, 2 * T], F32, name=f"raw{g}{u}", align_bytes=64)
-            both = raw[:].rearrange("p (e t) -> p e t", e=2)
-            for first, end, helper, by_helper in steps:
-                run = slice(T + first if first else 0, T + end)
-                nc.sync.dma_start(out=raw[:, run], in_=pair_rows[g, u, :, run])
-                if (g, u) == (0, 0):
-                    nc.sync.dma_start(picks[:], offs)
-                split = first + by_helper
-                for lo, hi, cast in ((first, split, helpers[helper]), (split, end, nc.scalar.copy)):
-                    cast(
-                        pairs[:, 2 * lo : 2 * hi].rearrange("p (c i e) -> p c e i", i=WALK, e=2),
-                        both[:, :, lo:hi].rearrange("p e (c i) -> p c e i", i=WALK),
-                    )
-            return pairs[:].bitcast(U32)
+        def gather_plane(plane, row, first, count):
+            nc.scalar.activation(plane, row[:].indirect(picks[:, cols(first, count)]), COPY)
 
-        def load_row(j, raw):
-            rounded = keep.tile([P, T], BF16, name=f"rounded{j}", align_bytes=64)
-            for first, width, by_gpsimd in ROW_LOADS[j]:
-                end, split = first + width, first + by_gpsimd
-                nc.sync.dma_start(out=raw[:, first:end], in_=single_rows[1, j, :, first:end])
-                gpsimd_round(rounded[:, first:split], raw[:, first:split])
-                if split < end:
-                    nc.scalar.copy(rounded[:, split:end], raw[:, split:end])
-            return rounded
+        def weave(woven, planes, lo, hi):
+            nc.vector.tensor_copy(
+                woven.rearrange("p (c i j) -> p c j i", i=WALK, j=PACK)[:, :, lo:hi, :],
+                planes[:, lo:hi, :].rearrange("p j (c i) -> p c j i", i=WALK),
+            )
 
-        def quantise(name, woven, widths):
-            codes = keep.tile([P, sum(widths)], U32, name=f"codes{name}", tag=f"codes{name}", align_bytes=64)
-            scales = keep.tile([P, sum(widths)], U8, name=f"scales{name}", align_bytes=64)
-            lo = 0
-            for width in widths:
-                nc.vector.quantize_mx(
-                    out=codes[:, lo : lo + width].bitcast(FP8X4),
-                    scales=scales[:, lo : lo + width],
-                    in_=woven[:, 2 * lo : 2 * (lo + width)].bitcast(BF16),
-                )
-                lo = lo + width
-            return [(codes[:, n : n + N_COLS], scales[:, n : n + N_COLS]) for n in range(0, lo, N_COLS)]
+        def quantise(codes, scales, woven):
+            nc.vector.quantize_mx(out=codes.bitcast(FP8X4), scales=scales, in_=woven)
 
-        woven0 = [keep.tile([P, S // 2, 2], U32, name=f"woven0_{h}", align_bytes=64) for h in range(2)]
-        halves0 = keep.tile([P, 2, S // 2], U32, name="halves0", align_bytes=64)
-        for u in range(2):
-            words0 = load_pair(0, u, PAIR_STEPS[u])
-            nc.vector.tensor_copy(halves0[:, u, :], words0.indirect(picks[:, entry_cols(S // 2, S // 2)]))
-            nc.vector.tensor_copy(woven0[0][:, :, u], words0.indirect(picks[:, entry_cols(0, S // 2)]))
-        nc.scalar.copy(
-            woven0[1][:].rearrange("p (c i) u -> p c u i", i=WALK),
-            halves0[:].rearrange("p u (c i) -> p c u i", i=WALK),
-        )
-        second_half = quantise("_pass0_1", woven0[1][:].rearrange("p s u -> p (s u)"), (S // 2,))
-        pass0 = quantise("_pass0_0", woven0[0][:].rearrange("p s u -> p (s u)"), (S // 2,)) + second_half
+        woven0 = [keep.tile([P, PACK * n], BF16, name=f"woven0_{n}_{h}", align_bytes=64) for h, n in enumerate((DIRECT0, S - DIRECT0))]
+        planes0 = keep.tile([P, PACK, S - DIRECT0], BF16, name="planes0", align_bytes=64)
+        codes0 = keep.tile([P, S], U32, name="codes0", align_bytes=64)
+        scales0 = keep.tile([P, S], U8, name="scales0", align_bytes=64)
+        for j in range(PACK):
+            row = load_row(0, j)
+            gather_woven(woven0[0][:], j, row, 0, DIRECT0)
+            gather_plane(planes0[:, j, :], row, DIRECT0, S - DIRECT0)
+        weave(woven0[1][:], planes0[:], 0, PACK)
+        quantise(codes0[:, 0:DIRECT0], scales0[:, 0:DIRECT0], woven0[0][:])
+        quantise(codes0[:, DIRECT0:S], scales0[:, DIRECT0:S], woven0[1][:])
 
-        words1 = load_pair(1, 0, PAIR_STEPS[2])
-        stage = keep.tile([P, STAGE], U32, name="stage", align_bytes=64)
-        lead = stage[:, LEAD : LEAD + 2 * LEAD_COUNT]
-        lead_rows = lead.bitcast(BF16).rearrange("p (s j) -> p s j", j=4)
-        lead_picks = picks[:, entry_cols(*PIECES[0])]
-        nc.vector.tensor_copy(lead.rearrange("p (s u) -> p s u", u=2)[:, :, 0], words1.indirect(lead_picks))
-
-        def gather_lower(first, count):
-            at = LOWER[1] + first - LEAD_COUNT
-            nc.vector.tensor_copy(stage[:, at : at + count], words1.indirect(picks[:, entry_cols(first, count)]))
-
-        def gather_upper(c, e, rounded):
-            upper = stage[:, UPPER[c] : UPPER[c] + COUNT].bitcast(BF16).rearrange("p (s e) -> p s e", e=2)
-            nc.scalar.activation(upper[:, :, e], rounded[:].indirect(picks[:, entry_cols(*PIECES[c])]), COPY)
-
-        gather_lower(LEAD_COUNT, S - LEAD_COUNT - LATE)
-        row2 = keep.tile([P, T], F32, name="row2", align_bytes=64)
-        rounded2 = load_row(2, row2[:])
-        nc.vector.tensor_copy(lead_rows[:, :, 2], row2[:].indirect(lead_picks))
-        gather_upper(1, 0, rounded2)
-        row3 = stage[:, ROW3 : ROW3 + T].bitcast(F32)
-        rounded3 = load_row(3, row3)
+        woven_a = keep.tile([P, PACK * LEAD], BF16, name="woven_a", align_bytes=64)
+        woven_b = keep.tile([P, PACK * COUNT], BF16, name="woven_b", align_bytes=64)
+        planes1 = keep.tile([P, PACK, 2 * COUNT], BF16, name="planes1", align_bytes=64)
+        for j in range(PACK):
+            row = load_row(1, j)
+            gather_woven(woven_a[:], j, row, *A)
+            if j < PACK - 1:
+                gather_plane(planes1[:, j, :], row, LEAD, 2 * COUNT)
+            else:
+                gather_plane(planes1[:, j, 0:COUNT], row, *B)
+                gather_plane(planes1[:, j, COUNT : 2 * COUNT], row, *C)
+            if j == 1:
+                weave(woven_b[:], planes1[:, :, 0:COUNT], 0, 2)
 
         w_words = keep.tile([P, PASSES, 2 * N], U8, name="w_words", align_bytes=64)
         nc.sync.dma_start(out=w_words[:].bitcast(I32), in_=w1_words.bitcast(I32).rearrange("g p n -> p g n"))
         nc.sync.dma_start(places[:], dst)
-        gates = []
-        for first, count in PIECES:
+        gates = {}
+        for piece in (A, B, C):
+            first, count = piece
             gate_sb = keep.tile([P, count], F32, name=f"gate{first}")
             nc.sync.dma_start(out=gate_sb[:], in_=gate[:, first : first + count])
-            gates.append(gate_sb[:])
-
-        def weave(c, tag):
-            both = stage[:, LOWER[c] : 2 * UPPER[c] - LOWER[c]].rearrange("p (u r) -> p u r", u=2)
-            woven = keep.tile([P, 2 * COUNT], U32, name=f"woven1_{c}", tag=tag, align_bytes=64)
-            for lo, hi in ((0, PARTS[0]), (PARTS[0], COUNT)):
-                nc.scalar.copy(
-                    woven[:, 2 * lo : 2 * hi].rearrange("p (c i u) -> p c u i", i=WALK, u=2),
-                    both[:, :, lo:hi].rearrange("p u (c i) -> p c u i", i=WALK),
-                )
-            return woven[:]
+            gates[piece] = gate_sb[:]
 
         pass1 = {}
 
-        def product(acc, c, b, lo):
-            for g, (codes, scales) in enumerate((pass0[(PIECES[c][0] + lo) // N_COLS], pass1[c][lo // N_COLS])):
+        def quantise1(piece, woven):
+            first, count = piece
+            codes = keep.tile([P, count], U32, name=f"codes1_{first}", align_bytes=64)
+            scales = keep.tile([P, count], U8, name=f"scales1_{first}", align_bytes=64)
+            quantise(codes[:], scales[:], woven)
+            pass1[piece] = (codes, scales)
+
+        def sums(piece, b):
+            first, count = piece
+            acc = psum.tile([P, count], F32, name=f"acc{first}_{b}")
+            parts = [(lo, min(256, count - lo)) for lo in range(0, count, 256)]
+            steps = [(g, lo, n) for g in range(PASSES) for lo, n in parts]
+            for i, (g, lo, n) in enumerate(steps):
+                codes, scales, at = (codes0, scales0, first + lo) if g == 0 else (*pass1[piece], lo)
                 nc.tensor.matmul_mx(
-                    out=acc,
+                    out=acc[:, lo : lo + n],
                     lhsT=w_words[:, g, 2 * P * b : 2 * P * (b + 1)].bitcast(FP4X4),
                     lhsT_scale=w_scales[:, g, P * b : P * (b + 1)],
-                    rhs=codes.bitcast(FP8X4),
-                    rhs_scale=scales,
-                    start=(g == 0),
-                    stop=(g == PASSES - 1),
+                    rhs=codes[:, at : at + n].bitcast(FP8X4),
+                    rhs_scale=scales[:, at : at + n],
+                    start=(i == 0),
+                    stop=(i == len(steps) - 1),
                 )
-
-        def block0_results(c):
-            count = PIECES[c][1]
-            y = keep.tile([P, count], F32, name=f"y{c}_0")
-            for lo in range(0, count, N_COLS):
-                acc = psum.tile([P, N_COLS], F32, name=f"acc{c}_{lo}", tag=f"first{lo}")
-                product(acc[:], c, 0, lo)
-                nc.scalar.activation(y[:, lo : lo + N_COLS], acc[:], GELU)
-            return y[:]
-
-        def block1_sums(c):
-            count = PIECES[c][1]
-            acc = psum.tile([P, count], F32, name=f"acc{c}_second", tag="second")
-            for lo in range(0, count, N_COLS):
-                product(acc[:, lo : lo + N_COLS], c, 1, lo)
             return acc[:]
 
-        def scatter(c, b, y):
-            nc.vector.tensor_tensor(windows[b][:].indirect(places[:, entry_cols(*PIECES[c])]), y, gates[c], MULT)
+        def gelu(piece, b, offset):
+            y = tail.tile([P, piece[1]], F32, name=f"y{piece[0]}_{b}", offset=offset)
+            nc.scalar.activation(y[:], sums(piece, b), GELU)
+            return y[:]
 
-        nc.vector.tensor_copy(lead_rows[:, :, 3], row3.indirect(lead_picks))
-        pass1[0] = quantise("0", lead, (LEAD_COUNT,))
-        gather_lower(S - LATE, LATE)
+        def weigh(piece, b, y, offset):
+            z = tail.tile([P, piece[1]], F32, name=f"z{piece[0]}_{b}", offset=offset)
+            nc.vector.tensor_tensor(z[:], y, gates[piece], MULT)
+            return z[:]
 
-        for c, (first, count) in enumerate(PIECES):
-            y0 = block0_results(c)
-            sums1 = block1_sums(c)
-            scatter(c, 0, y0)
-            if c + 1 < len(PIECES):
-                if c == 0:
-                    tag = "codes0"
-                else:
-                    tag = "woven2"
-                    gather_upper(c + 1, 0, rounded2)
-                gather_upper(c + 1, 1, rounded3)
-                pass1[c + 1] = quantise(f"{c + 1}", weave(c + 1, tag), PARTS)
-                end = LOWER[c + 1] + N_COLS
-                y1 = stage[:, end - count : end].bitcast(F32)
-            else:
-                y_last = keep.tile([P, count], F32, name="y_last")
-                y1 = y_last[:]
-            nc.scalar.activation(y1, sums1, GELU)
-            scatter(c, 1, y1)
+        def scatter_scalar(piece, b, z):
+            nc.scalar.activation(windows[b][:].indirect(places[:, cols(*piece)]), z, COPY)
+
+        def scatter_vector(piece, b, y):
+            nc.vector.tensor_tensor(windows[b][:].indirect(places[:, cols(*piece)]), y, gates[piece], MULT)
+
+        quantise1(A, woven_a[:])
+        weave(woven_b[:], planes1[:, :, 0:COUNT], 2, PACK)
+        quantise1(B, woven_b[:])
+        y_a0 = gelu(A, 0, 1024)
+        y_a1 = gelu(A, 1, 4096)
+        z_a0 = weigh(A, 0, y_a0, 5120)
+        scatter_scalar(A, 0, z_a0)
+        woven_c = tail.tile([P, PACK * COUNT], BF16, name="woven_c", offset=1024, align_bytes=64)
+        weave(woven_c[:], planes1[:, :, COUNT : 2 * COUNT], 0, PACK)
+        quantise1(C, woven_c[:])
+        z_a1 = weigh(A, 1, y_a1, 1536)
+        y_b0 = gelu(B, 0, 0)
+        y_b1 = gelu(B, 1, 2560)
+        y_c0 = gelu(C, 0, 6144)
+        scatter_vector(B, 0, y_b0)
+        scatter_scalar(A, 1, z_a1)
+        z_b1 = weigh(B, 1, y_b1, 7680)
+        y_c1 = gelu(C, 1, 9216)
+        scatter_vector(C, 0, y_c0)
+        scatter_scalar(B, 1, z_b1)
+        scatter_vector(C, 1, y_c1)
 
         for b in range(BLOCKS):
             nc.sync.dma_start(out=out[P * b : P * (b + 1), :], in_=windows[b][:])

@@ -50,11 +50,6 @@ def tile_picked_route2_lingelu_e_kernel(tc, xT, gate, w1_words, w1_scales, offs,
 
         w_scales = keep.tile([P, PASSES, N], U8, name="w_scales", align_bytes=64)
         nc.gpsimd.memset(w_scales[:], 0)
-        for q in range(4):
-            nc.gpsimd.dma_start(
-                out=w_scales[32 * q : 32 * q + 4].bitcast(I32),
-                in_=w1_scales.bitcast(I32)[:, 4 * q : 4 * q + 4, :].rearrange("g r n -> r g n"),
-            )
 
         rows = xT.rearrange("(g p j) t -> g j p t", g=PASSES, p=P, j=PACK)
 
@@ -98,7 +93,7 @@ def tile_picked_route2_lingelu_e_kernel(tc, xT, gate, w1_words, w1_scales, offs,
 
         woven_a = keep.tile([P, PACK * LEAD], BF16, name="woven_a", align_bytes=64)
         woven_b = keep.tile([P, PACK * COUNT], BF16, name="woven_b", align_bytes=64)
-        planes1 = keep.tile([P, PACK, 2 * COUNT], BF16, name="planes1", align_bytes=64)
+        planes1 = tail.tile([P, PACK, 2 * COUNT], BF16, name="planes1", align_bytes=64, offset=0)
         for j in range(PACK):
             row = load_row(1, j)
             gather_woven(woven_a[:], j, row, *A)
@@ -112,26 +107,32 @@ def tile_picked_route2_lingelu_e_kernel(tc, xT, gate, w1_words, w1_scales, offs,
 
         w_words = keep.tile([P, PASSES, 2 * N], U8, name="w_words", align_bytes=64)
         nc.sync.dma_start(out=w_words[:].bitcast(I32), in_=w1_words.bitcast(I32).rearrange("g p n -> p g n"))
-        nc.sync.dma_start(places[:], dst)
+        for q in range(4):
+            nc.sync.dma_start(
+                out=w_scales[32 * q : 32 * q + 4].bitcast(I32),
+                in_=w1_scales.bitcast(I32)[:, 4 * q : 4 * q + 4, :].rearrange("g r n -> r g n"),
+            )
         gates = {}
         for piece in (A, B, C):
             first, count = piece
             gate_sb = keep.tile([P, count], F32, name=f"gate{first}")
             nc.sync.dma_start(out=gate_sb[:], in_=gate[:, first : first + count])
             gates[piece] = gate_sb[:]
+            if piece == A:
+                nc.sync.dma_start(places[:], dst)
 
         pass1 = {}
 
-        def quantise1(piece, woven):
+        def quantise1(piece, woven, offset):
             first, count = piece
             codes = keep.tile([P, count], U32, name=f"codes1_{first}", align_bytes=64)
-            scales = keep.tile([P, count], U8, name=f"scales1_{first}", align_bytes=64)
+            scales = tail.tile([P, count], U8, name=f"scales1_{first}", align_bytes=64, offset=offset)
             quantise(codes[:], scales[:], woven)
             pass1[piece] = (codes, scales)
 
         def sums(piece, b):
             first, count = piece
-            acc = psum.tile([P, count], F32, name=f"acc{first}_{b}")
+            acc = psum.tile([P, count], F32, name=f"acc{first}_{b}", tag=f"bank{b}")
             parts = [(lo, min(256, count - lo)) for lo in range(0, count, 256)]
             steps = [(g, lo, n) for g in range(PASSES) for lo, n in parts]
             for i, (g, lo, n) in enumerate(steps):
@@ -163,24 +164,24 @@ def tile_picked_route2_lingelu_e_kernel(tc, xT, gate, w1_words, w1_scales, offs,
         def scatter_vector(piece, b, y):
             nc.vector.tensor_tensor(windows[b][:].indirect(places[:, cols(*piece)]), y, gates[piece], MULT)
 
-        quantise1(A, woven_a[:])
+        quantise1(A, woven_a[:], 16384)
         weave(woven_b[:], planes1[:, :, 0:COUNT], 2, PACK)
-        quantise1(B, woven_b[:])
-        y_a0 = gelu(A, 0, 1024)
-        y_a1 = gelu(A, 1, 4096)
-        z_a0 = weigh(A, 0, y_a0, 5120)
+        y_a0 = gelu(A, 0, 6144)
+        y_a1 = gelu(A, 1, 10240)
+        z_a0 = weigh(A, 0, y_a0, 11264)
         scatter_scalar(A, 0, z_a0)
-        woven_c = tail.tile([P, PACK * COUNT], BF16, name="woven_c", offset=1024, align_bytes=64)
+        quantise1(B, woven_b[:], 6144)
+        woven_c = tail.tile([P, PACK * COUNT], BF16, name="woven_c", offset=6656, align_bytes=64)
         weave(woven_c[:], planes1[:, :, COUNT : 2 * COUNT], 0, PACK)
-        quantise1(C, woven_c[:])
-        z_a1 = weigh(A, 1, y_a1, 1536)
-        y_b0 = gelu(B, 0, 0)
+        z_a1 = weigh(A, 1, y_a1, 0)
+        quantise1(C, woven_c[:], 16896)
+        y_b0 = gelu(B, 0, 1024)
         y_b1 = gelu(B, 1, 2560)
-        y_c0 = gelu(C, 0, 6144)
         scatter_vector(B, 0, y_b0)
         scatter_scalar(A, 1, z_a1)
-        z_b1 = weigh(B, 1, y_b1, 7680)
-        y_c1 = gelu(C, 1, 9216)
+        y_c0 = gelu(C, 0, 12288)
+        z_b1 = weigh(B, 1, y_b1, 13824)
+        y_c1 = gelu(C, 1, 17408)
         scatter_vector(C, 0, y_c0)
         scatter_scalar(B, 1, z_b1)
         scatter_vector(C, 1, y_c1)

@@ -23,10 +23,11 @@ PACK = 4
 BLOCKS = N // P
 PER_COL = 16
 WALK = 4
-DIRECT0 = S // 2
+DIRECT0 = 384
 
 LEAD = 256
 COUNT = (S - LEAD) // 2
+CUT = 288
 A, B, C = (0, LEAD), (LEAD, COUNT), (LEAD + COUNT, COUNT)
 
 
@@ -52,6 +53,7 @@ def tile_picked_route2_lingelu_e_kernel(tc, xT, gate, w1_words, w1_scales, offs,
         nc.gpsimd.memset(w_scales[:], 0)
 
         rows = xT.rearrange("(g p j) t -> g j p t", g=PASSES, p=P, j=PACK)
+        row_pairs = xT.rearrange("(g p u e) t -> g u p (e t)", g=PASSES, p=P, u=2, e=2)
 
         def cols(first, count):
             return slice(first // PER_COL, (first + count) // PER_COL)
@@ -59,16 +61,14 @@ def tile_picked_route2_lingelu_e_kernel(tc, xT, gate, w1_words, w1_scales, offs,
         def load_row(g, j):
             row = keep.tile([P, T], F32, name=f"row{g}{j}", align_bytes=64)
             nc.sync.dma_start(out=row[:], in_=rows[g, j])
-            if (g, j) == (0, 0):
-                nc.sync.dma_start(picks[:], offs)
-            return row
+            return row[:]
 
         def gather_woven(woven, j, row, first, count):
             slot = woven.rearrange("p (s j) -> p s j", j=PACK)[:, :, j]
-            nc.vector.tensor_copy(slot, row[:].indirect(picks[:, cols(first, count)]))
+            nc.vector.tensor_copy(slot, row.indirect(picks[:, cols(first, count)]))
 
         def gather_plane(plane, row, first, count):
-            nc.scalar.activation(plane, row[:].indirect(picks[:, cols(first, count)]), COPY)
+            nc.scalar.activation(plane, row.indirect(picks[:, cols(first, count)]), COPY)
 
         def weave(woven, planes, lo, hi):
             nc.vector.tensor_copy(
@@ -79,17 +79,21 @@ def tile_picked_route2_lingelu_e_kernel(tc, xT, gate, w1_words, w1_scales, offs,
         def quantise(codes, scales, woven):
             nc.vector.quantize_mx(out=codes.bitcast(FP8X4), scales=scales, in_=woven)
 
-        woven0 = [keep.tile([P, PACK * n], BF16, name=f"woven0_{n}_{h}", align_bytes=64) for h, n in enumerate((DIRECT0, S - DIRECT0))]
-        planes0 = keep.tile([P, PACK, S - DIRECT0], BF16, name="planes0", align_bytes=64)
+        woven0 = keep.tile([P, PACK * S], BF16, name="woven0", align_bytes=64)
+        planes0 = keep.tile([P, PACK, S - DIRECT0], F32, name="planes0", align_bytes=64)
         codes0 = keep.tile([P, S], U32, name="codes0", align_bytes=64)
         scales0 = keep.tile([P, S], U8, name="scales0", align_bytes=64)
-        for j in range(PACK):
-            row = load_row(0, j)
-            gather_woven(woven0[0][:], j, row, 0, DIRECT0)
-            gather_plane(planes0[:, j, :], row, DIRECT0, S - DIRECT0)
-        weave(woven0[1][:], planes0[:], 0, PACK)
-        quantise(codes0[:, 0:DIRECT0], scales0[:, 0:DIRECT0], woven0[0][:])
-        quantise(codes0[:, DIRECT0:S], scales0[:, DIRECT0:S], woven0[1][:])
+        for u in range(2):
+            pair = keep.tile([P, 2 * T], F32, name=f"pair{u}", align_bytes=64)
+            nc.sync.dma_start(out=pair[:], in_=row_pairs[0, u])
+            if u == 0:
+                nc.sync.dma_start(picks[:], offs)
+            for e in range(2):
+                row = pair[:, e * T : (e + 1) * T]
+                gather_woven(woven0[:, 0 : PACK * DIRECT0], 2 * u + e, row, 0, DIRECT0)
+                gather_plane(planes0[:, 2 * u + e, :], row, DIRECT0, S - DIRECT0)
+        weave(woven0[:, PACK * DIRECT0 : PACK * S], planes0[:], 0, PACK)
+        quantise(codes0[:], scales0[:], woven0[:])
 
         woven_a = keep.tile([P, PACK * LEAD], BF16, name="woven_a", align_bytes=64)
         woven_b = keep.tile([P, PACK * COUNT], BF16, name="woven_b", align_bytes=64)
@@ -112,31 +116,28 @@ def tile_picked_route2_lingelu_e_kernel(tc, xT, gate, w1_words, w1_scales, offs,
                 out=w_scales[32 * q : 32 * q + 4].bitcast(I32),
                 in_=w1_scales.bitcast(I32)[:, 4 * q : 4 * q + 4, :].rearrange("g r n -> r g n"),
             )
-        gates = {}
-        for piece in (A, B, C):
-            first, count = piece
-            gate_sb = keep.tile([P, count], F32, name=f"gate{first}")
-            nc.sync.dma_start(out=gate_sb[:], in_=gate[:, first : first + count])
-            gates[piece] = gate_sb[:]
-            if piece == A:
-                nc.sync.dma_start(places[:], dst)
+        gate_sb = keep.tile([P, S], F32, name="gate_sb")
+        nc.sync.dma_start(out=gate_sb[:], in_=gate)
+        nc.sync.dma_start(places[:], dst)
+        gates = {piece: gate_sb[:, piece[0] : piece[0] + piece[1]] for piece in (A, B, C)}
 
         pass1 = {}
 
-        def quantise1(piece, woven, offset):
+        def quantise1(piece, woven, offset, width):
             first, count = piece
             codes = keep.tile([P, count], U32, name=f"codes1_{first}", align_bytes=64)
             scales = tail.tile([P, count], U8, name=f"scales1_{first}", align_bytes=64, offset=offset)
-            quantise(codes[:], scales[:], woven)
+            for lo in range(0, count, width):
+                quantise(codes[:, lo : lo + width], scales[:, lo : lo + width], woven[:, PACK * lo : PACK * (lo + width)])
             pass1[piece] = (codes, scales)
 
-        def sums(piece, b):
-            first, count = piece
-            acc = psum.tile([P, count], F32, name=f"acc{first}_{b}", tag=f"bank{b}")
+        def sums(piece, b, start, count, bank):
+            first = piece[0] + start
+            acc = psum.tile([P, count], F32, name=f"acc{first}_{b}", tag=f"bank{bank}")
             parts = [(lo, min(256, count - lo)) for lo in range(0, count, 256)]
             steps = [(g, lo, n) for g in range(PASSES) for lo, n in parts]
             for i, (g, lo, n) in enumerate(steps):
-                codes, scales, at = (codes0, scales0, first + lo) if g == 0 else (*pass1[piece], lo)
+                codes, scales, at = (codes0, scales0, first + lo) if g == 0 else (*pass1[piece], start + lo)
                 nc.tensor.matmul_mx(
                     out=acc[:, lo : lo + n],
                     lhsT=w_words[:, g, 2 * P * b : 2 * P * (b + 1)].bitcast(FP4X4),
@@ -150,7 +151,7 @@ def tile_picked_route2_lingelu_e_kernel(tc, xT, gate, w1_words, w1_scales, offs,
 
         def gelu(piece, b, offset):
             y = tail.tile([P, piece[1]], F32, name=f"y{piece[0]}_{b}", offset=offset)
-            nc.scalar.activation(y[:], sums(piece, b), GELU)
+            nc.scalar.activation(y[:], sums(piece, b, 0, piece[1], b), GELU)
             return y[:]
 
         def weigh(piece, b, y, offset):
@@ -162,27 +163,36 @@ def tile_picked_route2_lingelu_e_kernel(tc, xT, gate, w1_words, w1_scales, offs,
             nc.scalar.activation(windows[b][:].indirect(places[:, cols(*piece)]), z, COPY)
 
         def scatter_vector(piece, b, y):
-            nc.vector.tensor_tensor(windows[b][:].indirect(places[:, cols(*piece)]), y, gates[piece], MULT)
+            first, count = piece
+            nc.vector.tensor_tensor(windows[b][:].indirect(places[:, cols(*piece)]), y, gate_sb[:, first : first + count], MULT)
 
-        quantise1(A, woven_a[:], 16384)
+        quantise1(A, woven_a[:], 16384, P)
         weave(woven_b[:], planes1[:, :, 0:COUNT], 2, PACK)
-        y_a0 = gelu(A, 0, 6144)
+        halves = []
+        for lo, bank, offset in ((0, 2, 6400), (P, 0, 19456)):
+            y_half = tail.tile([P, P], F32, name=f"y_lead{lo}", offset=offset)
+            nc.scalar.activation(y_half[:], sums(A, 0, lo, P, bank), GELU)
+            halves.append(y_half)
         y_a1 = gelu(A, 1, 10240)
-        z_a0 = weigh(A, 0, y_a0, 11264)
+        z_lead = keep.tile([P, LEAD], F32, name="z_lead")
+        z_a0 = z_lead[:]
+        for lo, y_half in zip((0, P), halves):
+            nc.vector.tensor_tensor(z_a0[:, lo : lo + P], y_half[:], gate_sb[:, lo : lo + P], MULT)
         scatter_scalar(A, 0, z_a0)
-        quantise1(B, woven_b[:], 6144)
+        quantise1(B, woven_b[:], 6144, COUNT)
         woven_c = tail.tile([P, PACK * COUNT], BF16, name="woven_c", offset=6656, align_bytes=64)
         weave(woven_c[:], planes1[:, :, COUNT : 2 * COUNT], 0, PACK)
         z_a1 = weigh(A, 1, y_a1, 0)
-        quantise1(C, woven_c[:], 16896)
-        y_b0 = gelu(B, 0, 1024)
-        y_b1 = gelu(B, 1, 2560)
-        scatter_vector(B, 0, y_b0)
+        quantise1(C, woven_c[:], 16896, COUNT)
+        y0 = tail.tile([P, 2 * COUNT], F32, name="y0", offset=1024)
+        nc.scalar.activation(y0[:, 0:COUNT], sums(B, 0, 0, COUNT, 0), GELU)
+        y_b1 = gelu(B, 1, 4096)
+        scatter_vector((LEAD, CUT), 0, y0[:, 0:CUT])
         scatter_scalar(A, 1, z_a1)
-        y_c0 = gelu(C, 0, 12288)
+        nc.scalar.activation(y0[:, COUNT : 2 * COUNT], sums(C, 0, 0, COUNT, 0), GELU)
         z_b1 = weigh(B, 1, y_b1, 13824)
         y_c1 = gelu(C, 1, 17408)
-        scatter_vector(C, 0, y_c0)
+        scatter_vector((LEAD + CUT, 2 * COUNT - CUT), 0, y0[:, CUT : 2 * COUNT])
         scatter_scalar(B, 1, z_b1)
         scatter_vector(C, 1, y_c1)
 

@@ -83,15 +83,13 @@ def tile_picked_route2_lingelu_e_kernel(tc, xT, gate, w1_words, w1_scales, offs,
         planes0 = keep.tile([P, PACK, S - DIRECT0], F32, name="planes0", align_bytes=64)
         codes0 = keep.tile([P, S], U32, name="codes0", align_bytes=64)
         scales0 = keep.tile([P, S], U8, name="scales0", align_bytes=64)
-        for u in range(2):
-            pair = keep.tile([P, 2 * T], F32, name=f"pair{u}", align_bytes=64)
-            nc.sync.dma_start(out=pair[:], in_=row_pairs[0, u])
-            if u == 0:
-                nc.sync.dma_start(picks[:], offs)
-            for e in range(2):
-                row = pair[:, e * T : (e + 1) * T]
-                gather_woven(woven0[:, 0 : PACK * DIRECT0], 2 * u + e, row, 0, DIRECT0)
-                gather_plane(planes0[:, 2 * u + e, :], row, DIRECT0, S - DIRECT0)
+        pair = keep.tile([P, 2 * T], F32, name="pair", align_bytes=64)
+        nc.sync.dma_start(out=pair[:], in_=row_pairs[0, 0])
+        nc.sync.dma_start(picks[:], offs)
+        for j in range(PACK):
+            row = pair[:, j * T : (j + 1) * T] if j < 2 else load_row(0, j)
+            gather_woven(woven0[:, 0 : PACK * DIRECT0], j, row, 0, DIRECT0)
+            gather_plane(planes0[:, j, :], row, DIRECT0, S - DIRECT0)
         weave(woven0[:, PACK * DIRECT0 : PACK * S], planes0[:], 0, PACK)
         quantise(codes0[:], scales0[:], woven0[:])
 
@@ -117,8 +115,9 @@ def tile_picked_route2_lingelu_e_kernel(tc, xT, gate, w1_words, w1_scales, offs,
                 in_=w1_scales.bitcast(I32)[:, 4 * q : 4 * q + 4, :].rearrange("g r n -> r g n"),
             )
         gate_sb = keep.tile([P, S], F32, name="gate_sb")
-        nc.sync.dma_start(out=gate_sb[:], in_=gate)
+        nc.sync.dma_start(out=gate_sb[:, 0:LEAD], in_=gate[:, 0:LEAD])
         nc.sync.dma_start(places[:], dst)
+        nc.sync.dma_start(out=gate_sb[:, LEAD:S], in_=gate[:, LEAD:S])
         gates = {piece: gate_sb[:, piece[0] : piece[0] + piece[1]] for piece in (A, B, C)}
 
         pass1 = {}

@@ -23,19 +23,29 @@ PACK = 4
 BLOCKS = N // P
 PER_COL = 16
 WALK = 4
-DIRECT0 = 384
+MOVING = 256
+DIRECT = 384
 
 LEAD = 256
+HALF = LEAD // 2
 COUNT = (S - LEAD) // 2
-CUT = 288
 A, B, C = (0, LEAD), (LEAD, COUNT), (LEAD + COUNT, COUNT)
+CUT = 288
+
+PLANES_AT = 0
+Z_A1_AT = PLANES_AT
+Y0_AT = Z_A1_AT + 4 * LEAD
+Y_B1_AT = Y0_AT + 4 * 2 * COUNT
+SCALES_B_AT = PLANES_AT + 2 * PACK * 2 * COUNT
+WOVEN_C_AT = SCALES_B_AT + 512
+Y_FIRST_AT = WOVEN_C_AT - 256
 
 
 def tile_picked_route2_lingelu_e_kernel(tc, xT, gate, w1_words, w1_scales, offs, dst, out):
     nc = tc.nc
     with ExitStack() as ctx:
         keep = ctx.enter_context(tc.tile_pool(name="keep", bufs=1))
-        tail = ctx.enter_context(tc.tile_pool(name="tail", bufs=1))
+        shared = ctx.enter_context(tc.tile_pool(name="shared", bufs=1))
         psum = ctx.enter_context(tc.psum_pool(name="psum", bufs=1))
 
         picks = keep.tile([P, S // PER_COL], U16, name="picks")
@@ -53,7 +63,6 @@ def tile_picked_route2_lingelu_e_kernel(tc, xT, gate, w1_words, w1_scales, offs,
         nc.gpsimd.memset(w_scales[:], 0)
 
         rows = xT.rearrange("(g p j) t -> g j p t", g=PASSES, p=P, j=PACK)
-        row_pairs = xT.rearrange("(g p u e) t -> g u p (e t)", g=PASSES, p=P, u=2, e=2)
 
         def cols(first, count):
             return slice(first // PER_COL, (first + count) // PER_COL)
@@ -80,32 +89,32 @@ def tile_picked_route2_lingelu_e_kernel(tc, xT, gate, w1_words, w1_scales, offs,
             nc.vector.quantize_mx(out=codes.bitcast(FP8X4), scales=scales, in_=woven)
 
         woven0 = keep.tile([P, PACK * S], BF16, name="woven0", align_bytes=64)
-        planes0 = keep.tile([P, PACK, S - DIRECT0], F32, name="planes0", align_bytes=64)
+        planes0 = keep.tile([P, PACK, S - DIRECT], BF16, name="planes0", align_bytes=64)
         codes0 = keep.tile([P, S], U32, name="codes0", align_bytes=64)
         scales0 = keep.tile([P, S], U8, name="scales0", align_bytes=64)
-        pair = keep.tile([P, 2 * T], F32, name="pair", align_bytes=64)
-        nc.sync.dma_start(out=pair[:], in_=row_pairs[0, 0])
-        nc.sync.dma_start(picks[:], offs)
         for j in range(PACK):
-            row = pair[:, j * T : (j + 1) * T] if j < 2 else load_row(0, j)
-            gather_woven(woven0[:, 0 : PACK * DIRECT0], j, row, 0, DIRECT0)
-            gather_plane(planes0[:, j, :], row, DIRECT0, S - DIRECT0)
-        weave(woven0[:, PACK * DIRECT0 : PACK * S], planes0[:], 0, PACK)
+            row = load_row(0, j)
+            if j == 0:
+                nc.sync.dma_start(picks[:], offs)
+            gather_woven(woven0[:, 0 : PACK * DIRECT], j, row, 0, DIRECT)
+            gather_plane(planes0[:, j, :], row, DIRECT, S - DIRECT)
+        weave(woven0[:, PACK * DIRECT : PACK * S], planes0[:], 0, PACK)
         quantise(codes0[:], scales0[:], woven0[:])
 
         woven_a = keep.tile([P, PACK * LEAD], BF16, name="woven_a", align_bytes=64)
         woven_b = keep.tile([P, PACK * COUNT], BF16, name="woven_b", align_bytes=64)
-        planes1 = tail.tile([P, PACK, 2 * COUNT], BF16, name="planes1", align_bytes=64, offset=0)
+        planes1 = shared.tile([P, PACK, 2 * COUNT], BF16, name="planes1", align_bytes=64, offset=PLANES_AT)
+        planes_b, planes_c = planes1[:, :, 0:COUNT], planes1[:, :, COUNT : 2 * COUNT]
         for j in range(PACK):
             row = load_row(1, j)
             gather_woven(woven_a[:], j, row, *A)
             if j < PACK - 1:
                 gather_plane(planes1[:, j, :], row, LEAD, 2 * COUNT)
             else:
-                gather_plane(planes1[:, j, 0:COUNT], row, *B)
-                gather_plane(planes1[:, j, COUNT : 2 * COUNT], row, *C)
+                gather_plane(planes_b[:, j, :], row, *B)
+                gather_plane(planes_c[:, j, :], row, *C)
             if j == 1:
-                weave(woven_b[:], planes1[:, :, 0:COUNT], 0, 2)
+                weave(woven_b[:], planes_b, 0, 2)
 
         w_words = keep.tile([P, PASSES, 2 * N], U8, name="w_words", align_bytes=64)
         nc.sync.dma_start(out=w_words[:].bitcast(I32), in_=w1_words.bitcast(I32).rearrange("g p n -> p g n"))
@@ -114,27 +123,25 @@ def tile_picked_route2_lingelu_e_kernel(tc, xT, gate, w1_words, w1_scales, offs,
                 out=w_scales[32 * q : 32 * q + 4].bitcast(I32),
                 in_=w1_scales.bitcast(I32)[:, 4 * q : 4 * q + 4, :].rearrange("g r n -> r g n"),
             )
-        gate_sb = keep.tile([P, S], F32, name="gate_sb")
-        nc.sync.dma_start(out=gate_sb[:, 0:LEAD], in_=gate[:, 0:LEAD])
+        gates = keep.tile([P, S], F32, name="gates")
+        nc.sync.dma_start(out=gates[:, 0:LEAD], in_=gate[:, 0:LEAD])
         nc.sync.dma_start(places[:], dst)
-        nc.sync.dma_start(out=gate_sb[:, LEAD:S], in_=gate[:, LEAD:S])
-        gates = {piece: gate_sb[:, piece[0] : piece[0] + piece[1]] for piece in (A, B, C)}
+        nc.sync.dma_start(out=gates[:, LEAD:S], in_=gate[:, LEAD:S])
 
         pass1 = {}
 
-        def quantise1(piece, woven, offset, width):
+        def quantise_piece(piece, scales, woven, width):
             first, count = piece
             codes = keep.tile([P, count], U32, name=f"codes1_{first}", align_bytes=64)
-            scales = tail.tile([P, count], U8, name=f"scales1_{first}", align_bytes=64, offset=offset)
             for lo in range(0, count, width):
-                quantise(codes[:, lo : lo + width], scales[:, lo : lo + width], woven[:, PACK * lo : PACK * (lo + width)])
+                hi = lo + width
+                quantise(codes[:, lo:hi], scales[:, lo:hi], woven[:, PACK * lo : PACK * hi])
             pass1[piece] = (codes, scales)
 
-        def sums(piece, b, start, count, bank):
+        def gelu(y, piece, b, start, count, bank):
             first = piece[0] + start
             acc = psum.tile([P, count], F32, name=f"acc{first}_{b}", tag=f"bank{bank}")
-            parts = [(lo, min(256, count - lo)) for lo in range(0, count, 256)]
-            steps = [(g, lo, n) for g in range(PASSES) for lo, n in parts]
+            steps = [(g, lo, min(MOVING, count - lo)) for g in range(PASSES) for lo in range(0, count, MOVING)]
             for i, (g, lo, n) in enumerate(steps):
                 codes, scales, at = (codes0, scales0, first + lo) if g == 0 else (*pass1[piece], start + lo)
                 nc.tensor.matmul_mx(
@@ -146,54 +153,55 @@ def tile_picked_route2_lingelu_e_kernel(tc, xT, gate, w1_words, w1_scales, offs,
                     start=(i == 0),
                     stop=(i == len(steps) - 1),
                 )
-            return acc[:]
+            nc.scalar.activation(y, acc[:], GELU)
 
-        def gelu(piece, b, offset):
-            y = tail.tile([P, piece[1]], F32, name=f"y{piece[0]}_{b}", offset=offset)
-            nc.scalar.activation(y[:], sums(piece, b, 0, piece[1], b), GELU)
-            return y[:]
+        def weigh(z, y, first, count):
+            nc.vector.tensor_tensor(z, y, gates[:, first : first + count], MULT)
 
-        def weigh(piece, b, y, offset):
-            z = tail.tile([P, piece[1]], F32, name=f"z{piece[0]}_{b}", offset=offset)
-            nc.vector.tensor_tensor(z[:], y, gates[piece], MULT)
-            return z[:]
+        def scatter_on_scalar(b, z, first, count):
+            nc.scalar.activation(windows[b][:].indirect(places[:, cols(first, count)]), z, COPY)
 
-        def scatter_scalar(piece, b, z):
-            nc.scalar.activation(windows[b][:].indirect(places[:, cols(*piece)]), z, COPY)
+        def scatter_on_vector(b, y, first, count):
+            weigh(windows[b][:].indirect(places[:, cols(first, count)]), y, first, count)
 
-        def scatter_vector(piece, b, y):
-            first, count = piece
-            nc.vector.tensor_tensor(windows[b][:].indirect(places[:, cols(*piece)]), y, gate_sb[:, first : first + count], MULT)
+        scales_a = keep.tile([P, LEAD], U8, name="scales_a", align_bytes=64)
+        quantise_piece(A, scales_a, woven_a[:], HALF)
+        weave(woven_b[:], planes_b, 2, PACK)
+        y_first = shared.tile([P, HALF], F32, name="y_first", offset=Y_FIRST_AT)
+        y_second = keep.tile([P, HALF], F32, name="y_second")
+        y_a1 = keep.tile([P, LEAD], F32, name="y_a1")
+        z_a0 = keep.tile([P, LEAD], F32, name="z_a0")
+        gelu(y_first[:], A, 0, 0, HALF, 2)
+        gelu(y_second[:], A, 0, HALF, HALF, 0)
+        gelu(y_a1[:], A, 1, 0, LEAD, 1)
+        weigh(z_a0[:, 0:HALF], y_first[:], 0, HALF)
+        weigh(z_a0[:, HALF:LEAD], y_second[:], HALF, HALF)
+        scatter_on_scalar(0, z_a0[:], *A)
 
-        quantise1(A, woven_a[:], 16384, P)
-        weave(woven_b[:], planes1[:, :, 0:COUNT], 2, PACK)
-        halves = []
-        for lo, bank, offset in ((0, 2, 6400), (P, 0, 19456)):
-            y_half = tail.tile([P, P], F32, name=f"y_lead{lo}", offset=offset)
-            nc.scalar.activation(y_half[:], sums(A, 0, lo, P, bank), GELU)
-            halves.append(y_half)
-        y_a1 = gelu(A, 1, 10240)
-        z_lead = keep.tile([P, LEAD], F32, name="z_lead")
-        z_a0 = z_lead[:]
-        for lo, y_half in zip((0, P), halves):
-            nc.vector.tensor_tensor(z_a0[:, lo : lo + P], y_half[:], gate_sb[:, lo : lo + P], MULT)
-        scatter_scalar(A, 0, z_a0)
-        quantise1(B, woven_b[:], 6144, COUNT)
-        woven_c = tail.tile([P, PACK * COUNT], BF16, name="woven_c", offset=6656, align_bytes=64)
-        weave(woven_c[:], planes1[:, :, COUNT : 2 * COUNT], 0, PACK)
-        z_a1 = weigh(A, 1, y_a1, 0)
-        quantise1(C, woven_c[:], 16896, COUNT)
-        y0 = tail.tile([P, 2 * COUNT], F32, name="y0", offset=1024)
-        nc.scalar.activation(y0[:, 0:COUNT], sums(B, 0, 0, COUNT, 0), GELU)
-        y_b1 = gelu(B, 1, 4096)
-        scatter_vector((LEAD, CUT), 0, y0[:, 0:CUT])
-        scatter_scalar(A, 1, z_a1)
-        nc.scalar.activation(y0[:, COUNT : 2 * COUNT], sums(C, 0, 0, COUNT, 0), GELU)
-        z_b1 = weigh(B, 1, y_b1, 13824)
-        y_c1 = gelu(C, 1, 17408)
-        scatter_vector((LEAD + CUT, 2 * COUNT - CUT), 0, y0[:, CUT : 2 * COUNT])
-        scatter_scalar(B, 1, z_b1)
-        scatter_vector(C, 1, y_c1)
+        scales_b = shared.tile([P, COUNT], U8, name="scales_b", align_bytes=64, offset=SCALES_B_AT)
+        quantise_piece(B, scales_b, woven_b[:], COUNT)
+        woven_c = shared.tile([P, PACK * COUNT], BF16, name="woven_c", align_bytes=64, offset=WOVEN_C_AT)
+        weave(woven_c[:], planes_c, 0, PACK)
+
+        z_a1 = shared.tile([P, LEAD], F32, name="z_a1", offset=Z_A1_AT)
+        weigh(z_a1[:], y_a1[:], *A)
+        scales_c = keep.tile([P, COUNT], U8, name="scales_c", align_bytes=64)
+        quantise_piece(C, scales_c, woven_c[:], COUNT)
+        y0 = shared.tile([P, 2 * COUNT], F32, name="y0", offset=Y0_AT)
+        y_b1 = shared.tile([P, COUNT], F32, name="y_b1", offset=Y_B1_AT)
+        gelu(y0[:, 0:COUNT], B, 0, 0, COUNT, 0)
+        gelu(y_b1[:], B, 1, 0, COUNT, 1)
+        scatter_on_vector(0, y0[:, 0:CUT], LEAD, CUT)
+        scatter_on_scalar(1, z_a1[:], *A)
+
+        z_b1 = keep.tile([P, COUNT], F32, name="z_b1")
+        y_c1 = keep.tile([P, COUNT], F32, name="y_c1")
+        gelu(y0[:, COUNT : 2 * COUNT], C, 0, 0, COUNT, 0)
+        weigh(z_b1[:], y_b1[:], *B)
+        gelu(y_c1[:], C, 1, 0, COUNT, 1)
+        scatter_on_vector(0, y0[:, CUT : 2 * COUNT], LEAD + CUT, 2 * COUNT - CUT)
+        scatter_on_scalar(1, z_b1[:], *B)
+        scatter_on_vector(1, y_c1[:], *C)
 
         for b in range(BLOCKS):
             nc.sync.dma_start(out=out[P * b : P * (b + 1), :], in_=windows[b][:])

@@ -22,7 +22,7 @@ PASSES = K // 512
 PACK = 4
 BLOCKS = N // P
 PER_COL = 16
-WALK = 4
+LINE = 16
 MOVING = 256
 DIRECT = 384
 
@@ -63,6 +63,7 @@ def tile_picked_route2_lingelu_e_kernel(tc, xT, gate, w1_words, w1_scales, offs,
         nc.gpsimd.memset(w_scales[:], 0)
 
         rows = xT.rearrange("(g p j) t -> g j p t", g=PASSES, p=P, j=PACK)
+        row_pairs = xT.rearrange("(g p u e) t -> g u p (e t)", g=PASSES, p=P, u=2, e=2)
 
         def cols(first, count):
             return slice(first // PER_COL, (first + count) // PER_COL)
@@ -80,22 +81,24 @@ def tile_picked_route2_lingelu_e_kernel(tc, xT, gate, w1_words, w1_scales, offs,
             nc.scalar.activation(plane, row.indirect(picks[:, cols(first, count)]), COPY)
 
         def weave(woven, planes, lo, hi):
+            walk = LINE // (4 if planes.dtype == F32 else 2)
             nc.vector.tensor_copy(
-                woven.rearrange("p (c i j) -> p c j i", i=WALK, j=PACK)[:, :, lo:hi, :],
-                planes[:, lo:hi, :].rearrange("p j (c i) -> p c j i", i=WALK),
+                woven.rearrange("p (c i j) -> p c j i", i=walk, j=PACK)[:, :, lo:hi, :],
+                planes[:, lo:hi, :].rearrange("p j (c i) -> p c j i", i=walk),
             )
 
         def quantise(codes, scales, woven):
             nc.vector.quantize_mx(out=codes.bitcast(FP8X4), scales=scales, in_=woven)
 
         woven0 = keep.tile([P, PACK * S], BF16, name="woven0", align_bytes=64)
-        planes0 = keep.tile([P, PACK, S - DIRECT], BF16, name="planes0", align_bytes=64)
+        planes0 = keep.tile([P, PACK, S - DIRECT], F32, name="planes0", align_bytes=64)
         codes0 = keep.tile([P, S], U32, name="codes0", align_bytes=64)
         scales0 = keep.tile([P, S], U8, name="scales0", align_bytes=64)
+        pair = keep.tile([P, 2 * T], F32, name="pair", align_bytes=64)
+        nc.sync.dma_start(out=pair[:], in_=row_pairs[0, 0])
+        nc.sync.dma_start(picks[:], offs)
         for j in range(PACK):
-            row = load_row(0, j)
-            if j == 0:
-                nc.sync.dma_start(picks[:], offs)
+            row = pair[:, j * T : (j + 1) * T] if j < 2 else load_row(0, j)
             gather_woven(woven0[:, 0 : PACK * DIRECT], j, row, 0, DIRECT)
             gather_plane(planes0[:, j, :], row, DIRECT, S - DIRECT)
         weave(woven0[:, PACK * DIRECT : PACK * S], planes0[:], 0, PACK)

@@ -23,22 +23,11 @@ PACK = 4
 BLOCKS = N // P
 PER_COL = 16
 LINE = 16
-MOVING = 256
 DIRECT = 384
 
-LEAD = 256
-HALF = LEAD // 2
-COUNT = (S - LEAD) // 2
-A, B, C = (0, LEAD), (LEAD, COUNT), (LEAD + COUNT, COUNT)
-CUT = 288
-
-PLANES_AT = 0
-Z_A1_AT = PLANES_AT
-Y0_AT = Z_A1_AT + 4 * LEAD
-Y_B1_AT = Y0_AT + 4 * 2 * COUNT
-SCALES_B_AT = PLANES_AT + 2 * PACK * 2 * COUNT
-WOVEN_C_AT = SCALES_B_AT + 512
-Y_FIRST_AT = WOVEN_C_AT - 256
+PIECE = 256
+HALF = PIECE // 2
+A, B, C, D = range(0, S, PIECE)
 
 
 def tile_picked_route2_lingelu_e_kernel(tc, xT, gate, w1_words, w1_scales, offs, dst, out):
@@ -80,9 +69,9 @@ def tile_picked_route2_lingelu_e_kernel(tc, xT, gate, w1_words, w1_scales, offs,
         def gather_plane(plane, row, first, count):
             nc.scalar.activation(plane, row.indirect(picks[:, cols(first, count)]), COPY)
 
-        def weave(woven, planes, lo, hi):
+        def weave(woven, planes, lo, hi, copy=nc.vector.tensor_copy):
             walk = LINE // (4 if planes.dtype == F32 else 2)
-            nc.vector.tensor_copy(
+            copy(
                 woven.rearrange("p (c i j) -> p c j i", i=walk, j=PACK)[:, :, lo:hi, :],
                 planes[:, lo:hi, :].rearrange("p j (c i) -> p c j i", i=walk),
             )
@@ -104,20 +93,21 @@ def tile_picked_route2_lingelu_e_kernel(tc, xT, gate, w1_words, w1_scales, offs,
         weave(woven0[:, PACK * DIRECT : PACK * S], planes0[:], 0, PACK)
         quantise(codes0[:], scales0[:], woven0[:])
 
-        woven_a = keep.tile([P, PACK * LEAD], BF16, name="woven_a", align_bytes=64)
-        woven_b = keep.tile([P, PACK * COUNT], BF16, name="woven_b", align_bytes=64)
-        planes1 = shared.tile([P, PACK, 2 * COUNT], BF16, name="planes1", align_bytes=64, offset=PLANES_AT)
-        planes_b, planes_c = planes1[:, :, 0:COUNT], planes1[:, :, COUNT : 2 * COUNT]
+        woven_a = keep.tile([P, PACK * PIECE], BF16, name="woven_a", align_bytes=64)
+        woven_bc = keep.tile([P, PACK * 2 * PIECE], BF16, name="woven_bc", align_bytes=64)
+        woven_b, woven_c = woven_bc[:, 0 : PACK * PIECE], woven_bc[:, PACK * PIECE :]
+        planes1 = keep.tile([P, PACK, 3 * PIECE], BF16, name="planes1", align_bytes=64)
+        planes = {first: planes1[:, :, first - B : first - B + PIECE] for first in (B, C, D)}
         for j in range(PACK):
             row = load_row(1, j)
-            gather_woven(woven_a[:], j, row, *A)
+            gather_woven(woven_a[:], j, row, A, PIECE)
             if j < PACK - 1:
-                gather_plane(planes1[:, j, :], row, LEAD, 2 * COUNT)
+                gather_plane(planes1[:, j, :], row, B, 3 * PIECE)
             else:
-                gather_plane(planes_b[:, j, :], row, *B)
-                gather_plane(planes_c[:, j, :], row, *C)
+                for first in (B, C, D):
+                    gather_plane(planes[first][:, j, :], row, first, PIECE)
             if j == 1:
-                weave(woven_b[:], planes_b, 0, 2)
+                weave(woven_bc[:], planes1[:, :, 0 : 2 * PIECE], 0, 2)
 
         w_words = keep.tile([P, PASSES, 2 * N], U8, name="w_words", align_bytes=64)
         nc.sync.dma_start(out=w_words[:].bitcast(I32), in_=w1_words.bitcast(I32).rearrange("g p n -> p g n"))
@@ -127,84 +117,98 @@ def tile_picked_route2_lingelu_e_kernel(tc, xT, gate, w1_words, w1_scales, offs,
                 in_=w1_scales.bitcast(I32)[:, 4 * q : 4 * q + 4, :].rearrange("g r n -> r g n"),
             )
         gates = keep.tile([P, S], F32, name="gates")
-        nc.sync.dma_start(out=gates[:, 0:LEAD], in_=gate[:, 0:LEAD])
+        nc.sync.dma_start(out=gates[:, 0:PIECE], in_=gate[:, 0:PIECE])
         nc.sync.dma_start(places[:], dst)
-        nc.sync.dma_start(out=gates[:, LEAD:S], in_=gate[:, LEAD:S])
+        for first in range(PIECE, S, HALF):
+            nc.sync.dma_start(out=gates[:, first : first + HALF], in_=gate[:, first : first + HALF])
 
         pass1 = {}
 
-        def quantise_piece(piece, scales, woven, width):
-            first, count = piece
-            codes = keep.tile([P, count], U32, name=f"codes1_{first}", align_bytes=64)
-            for lo in range(0, count, width):
-                hi = lo + width
-                quantise(codes[:, lo:hi], scales[:, lo:hi], woven[:, PACK * lo : PACK * hi])
-            pass1[piece] = (codes, scales)
+        def quantise1(first, count, woven, pool=keep, **place):
+            codes = pool.tile([P, count], U32, name=f"codes1_{first}", align_bytes=64, **place)
+            scales = keep.tile([P, count], U8, name=f"scales1_{first}", align_bytes=64)
+            quantise(codes[:], scales[:], woven)
+            for lo in range(0, count, PIECE):
+                n = min(count, PIECE)
+                pass1[first + lo] = (codes[:, lo : lo + n], scales[:, lo : lo + n])
 
-        def gelu(y, piece, b, start, count, bank):
-            first = piece[0] + start
-            acc = psum.tile([P, count], F32, name=f"acc{first}_{b}", tag=f"bank{bank}")
-            steps = [(g, lo, min(MOVING, count - lo)) for g in range(PASSES) for lo in range(0, count, MOVING)]
-            for i, (g, lo, n) in enumerate(steps):
-                codes, scales, at = (codes0, scales0, first + lo) if g == 0 else (*pass1[piece], start + lo)
+        def group(y, b, steps, bank):
+            count = sum(n for first, n in steps)
+            acc = psum.tile([P, count], F32, name=f"acc{steps[0][0]}_{b}", tag=f"bank{bank}")
+            calls = [(0, steps[0][0], count)] + [(1, first, n) for first, n in steps]
+
+            def matmul(i):
+                g, first, n = calls[i]
+                codes, scales = (codes0[:, first : first + n], scales0[:, first : first + n]) if g == 0 else pass1[first]
+                lo = first - steps[0][0]
                 nc.tensor.matmul_mx(
                     out=acc[:, lo : lo + n],
                     lhsT=w_words[:, g, 2 * P * b : 2 * P * (b + 1)].bitcast(FP4X4),
                     lhsT_scale=w_scales[:, g, P * b : P * (b + 1)],
-                    rhs=codes[:, at : at + n].bitcast(FP8X4),
-                    rhs_scale=scales[:, at : at + n],
+                    rhs=codes.bitcast(FP8X4),
+                    rhs_scale=scales,
                     start=(i == 0),
-                    stop=(i == len(steps) - 1),
+                    stop=(i == len(calls) - 1),
                 )
-            nc.scalar.activation(y, acc[:], GELU)
 
-        def weigh(z, y, first, count):
-            nc.vector.tensor_tensor(z, y, gates[:, first : first + count], MULT)
+            def rest():
+                for i in range(1, len(calls)):
+                    matmul(i)
+                nc.scalar.activation(y, acc[:], GELU)
 
-        def scatter_on_scalar(b, z, first, count):
-            nc.scalar.activation(windows[b][:].indirect(places[:, cols(first, count)]), z, COPY)
+            matmul(0)
+            return rest
 
-        def scatter_on_vector(b, y, first, count):
-            weigh(windows[b][:].indirect(places[:, cols(first, count)]), y, first, count)
+        ys = [keep.tile([P, S], F32, name=f"y{b}") for b in range(BLOCKS)]
+        z1 = keep.tile([P, D], F32, name="z1")
 
-        scales_a = keep.tile([P, LEAD], U8, name="scales_a", align_bytes=64)
-        quantise_piece(A, scales_a, woven_a[:], HALF)
-        weave(woven_b[:], planes_b, 2, PACK)
-        y_first = shared.tile([P, HALF], F32, name="y_first", offset=Y_FIRST_AT)
-        y_second = keep.tile([P, HALF], F32, name="y_second")
-        y_a1 = keep.tile([P, LEAD], F32, name="y_a1")
-        z_a0 = keep.tile([P, LEAD], F32, name="z_a0")
-        gelu(y_first[:], A, 0, 0, HALF, 2)
-        gelu(y_second[:], A, 0, HALF, HALF, 0)
-        gelu(y_a1[:], A, 1, 0, LEAD, 1)
-        weigh(z_a0[:, 0:HALF], y_first[:], 0, HALF)
-        weigh(z_a0[:, HALF:LEAD], y_second[:], HALF, HALF)
-        scatter_on_scalar(0, z_a0[:], *A)
+        def gelu_piece(b, first, bank):
+            group(ys[b][:, first : first + PIECE], b, [(first, PIECE)], bank)()
 
-        scales_b = shared.tile([P, COUNT], U8, name="scales_b", align_bytes=64, offset=SCALES_B_AT)
-        quantise_piece(B, scales_b, woven_b[:], COUNT)
-        woven_c = shared.tile([P, PACK * COUNT], BF16, name="woven_c", align_bytes=64, offset=WOVEN_C_AT)
-        weave(woven_c[:], planes_c, 0, PACK)
+        def weigh(z, b, first, count=PIECE):
+            nc.vector.tensor_tensor(z, ys[b][:, first : first + count], gates[:, first : first + count], MULT)
 
-        z_a1 = shared.tile([P, LEAD], F32, name="z_a1", offset=Z_A1_AT)
-        weigh(z_a1[:], y_a1[:], *A)
-        scales_c = keep.tile([P, COUNT], U8, name="scales_c", align_bytes=64)
-        quantise_piece(C, scales_c, woven_c[:], COUNT)
-        y0 = shared.tile([P, 2 * COUNT], F32, name="y0", offset=Y0_AT)
-        y_b1 = shared.tile([P, COUNT], F32, name="y_b1", offset=Y_B1_AT)
-        gelu(y0[:, 0:COUNT], B, 0, 0, COUNT, 0)
-        gelu(y_b1[:], B, 1, 0, COUNT, 1)
-        scatter_on_vector(0, y0[:, 0:CUT], LEAD, CUT)
-        scatter_on_scalar(1, z_a1[:], *A)
+        def weigh1(first):
+            weigh(z1[:, first : first + PIECE], 1, first)
 
-        z_b1 = keep.tile([P, COUNT], F32, name="z_b1")
-        y_c1 = keep.tile([P, COUNT], F32, name="y_c1")
-        gelu(y0[:, COUNT : 2 * COUNT], C, 0, 0, COUNT, 0)
-        weigh(z_b1[:], y_b1[:], *B)
-        gelu(y_c1[:], C, 1, 0, COUNT, 1)
-        scatter_on_vector(0, y0[:, CUT : 2 * COUNT], LEAD + CUT, 2 * COUNT - CUT)
-        scatter_on_scalar(1, z_b1[:], *B)
-        scatter_on_vector(1, y_c1[:], *C)
+        def scatter_on_scalar(first):
+            nc.scalar.activation(windows[1][:].indirect(places[:, cols(first, PIECE)]), z1[:, first : first + PIECE], COPY)
+
+        def scatter_on_vector(b, first, count=PIECE):
+            weigh(windows[b][:].indirect(places[:, cols(first, count)]), b, first, count)
+
+        quantise1(0, HALF, woven_a[:, 0 : PACK * HALF])
+        quantise1(HALF, HALF, woven_a[:, PACK * HALF :], shared, offset=0)
+        weave(woven_b, planes[B], 2, PACK)
+        weave(woven_c, planes[C], 2, PACK)
+        quantise1(B, PIECE, woven_b)
+        quantise1(C, PIECE, woven_c)
+        lead = [
+            group(ys[0][:, 0:HALF], 0, [(0, HALF)], 0),
+            group(ys[0][:, HALF:PIECE], 0, [(HALF, HALF)], 1),
+            group(ys[1][:, 0:PIECE], 1, [(0, HALF), (HALF, HALF)], 2),
+        ]
+        for rest in lead:
+            rest()
+        scatter_on_vector(0, A)
+        weigh1(A)
+        woven_d = shared.tile([P, PACK * PIECE], BF16, name="woven_d", align_bytes=64, offset=0)
+        weave(woven_d[:], planes[D], 0, PACK, nc.scalar.copy)
+        gelu_piece(1, B, 4)
+        gelu_piece(0, B, 3)
+        gelu_piece(0, C, 5)
+        gelu_piece(1, C, 6)
+        scatter_on_scalar(A)
+        quantise1(D, PIECE, woven_d[:])
+        weigh1(B)
+        scatter_on_vector(0, B)
+        weigh1(C)
+        gelu_piece(0, D, 7)
+        scatter_on_scalar(B)
+        gelu_piece(1, D, 0)
+        scatter_on_vector(0, C, 2 * PIECE)
+        scatter_on_scalar(C)
+        scatter_on_vector(1, D)
 
         for b in range(BLOCKS):
             nc.sync.dma_start(out=out[P * b : P * (b + 1), :], in_=windows[b][:])

@@ -28,6 +28,7 @@ DIRECT = 384
 PIECE = 256
 HALF = PIECE // 2
 A, B, C, D = range(0, S, PIECE)
+SPARE = 96
 
 
 def tile_picked_route2_lingelu_e_kernel(tc, xT, gate, w1_words, w1_scales, offs, dst, out):
@@ -104,13 +105,16 @@ def tile_picked_route2_lingelu_e_kernel(tc, xT, gate, w1_words, w1_scales, offs,
             if j < PACK - 1:
                 gather_plane(planes1[:, j, :], row, B, 3 * PIECE)
             else:
+                nc.vector.tensor_copy(planes[D][:, j, PIECE - SPARE :], row.indirect(picks[:, cols(S - SPARE, SPARE)]))
                 for first in (B, C, D):
-                    gather_plane(planes[first][:, j, :], row, first, PIECE)
+                    count = min(PIECE, S - SPARE - first)
+                    gather_plane(planes[first][:, j, 0:count], row, first, count)
             if j == 1:
                 weave(woven_bc[:], planes1[:, :, 0 : 2 * PIECE], 0, 2)
 
         w_words = keep.tile([P, PASSES, 2 * N], U8, name="w_words", align_bytes=64)
-        nc.sync.dma_start(out=w_words[:].bitcast(I32), in_=w1_words.bitcast(I32).rearrange("g p n -> p g n"))
+        for g in range(PASSES):
+            nc.sync.dma_start(out=w_words[:, g, :].bitcast(I32), in_=w1_words.bitcast(I32)[g])
         for q in range(4):
             nc.sync.dma_start(
                 out=w_scales[32 * q : 32 * q + 4].bitcast(I32),
@@ -119,8 +123,8 @@ def tile_picked_route2_lingelu_e_kernel(tc, xT, gate, w1_words, w1_scales, offs,
         gates = keep.tile([P, S], F32, name="gates")
         nc.sync.dma_start(out=gates[:, 0:PIECE], in_=gate[:, 0:PIECE])
         nc.sync.dma_start(places[:], dst)
-        for first in range(PIECE, S, HALF):
-            nc.sync.dma_start(out=gates[:, first : first + HALF], in_=gate[:, first : first + HALF])
+        for first, count in ((B, HALF), (B + HALF, HALF), (C, HALF), (C + HALF, HALF), (D, PIECE)):
+            nc.sync.dma_start(out=gates[:, first : first + count], in_=gate[:, first : first + count])
 
         pass1 = {}
 

from contextlib import ExitStack

import concourse.mybir as mybir

K, T, S, N, U = 1024, 2048, 1024, 256, 2048
FLOPS = 2 * K * N * S

F32 = mybir.dt.float32
BF16 = mybir.dt.bfloat16
I32 = mybir.dt.int32
U32 = mybir.dt.uint32
U16 = mybir.dt.uint16
U8 = mybir.dt.uint8
FP8X4 = mybir.dt.float8_e4m3fn_x4
FP4X4 = mybir.dt.float4_e2m1fn_x4
GELU = mybir.ActivationFunctionType.Gelu_apprx_tanh
COPY = mybir.ActivationFunctionType.Copy
MULT = mybir.AluOpType.mult

P = 128
PASSES = K // 512
PACK = 4
BLOCKS = N // P
PER_COL = 16
LINE = 16
DIRECT = 384

PIECE = 256
HALF = PIECE // 2
A, B, C, D = range(0, S, PIECE)
SPARE = 96


def tile_picked_route2_lingelu_e_kernel(tc, xT, gate, w1_words, w1_scales, offs, dst, out):
    nc = tc.nc
    with ExitStack() as ctx:
        keep = ctx.enter_context(tc.tile_pool(name="keep", bufs=1))
        shared = ctx.enter_context(tc.tile_pool(name="shared", bufs=1))
        psum = ctx.enter_context(tc.psum_pool(name="psum", bufs=1))

        picks = keep.tile([P, S // PER_COL], U16, name="picks")
        places = keep.tile([P, S // PER_COL], U16, name="places")

        windows = [keep.tile([P, U], F32, name=f"window{b}") for b in range(BLOCKS)]
        for window in windows:
            nc.vector.memset(window[:], 0.0)

        warm = keep.tile([P, 16], F32, name="warm")
        nc.gpsimd.memset(warm[:, 0:8], 0.0)
        nc.scalar.activation(warm[:, 8:16], warm[:, 0:8], GELU)

        w_scales = keep.tile([P, PASSES, N], U8, name="w_scales", align_bytes=64)
        nc.gpsimd.memset(w_scales[:], 0)

        rows = xT.rearrange("(g p j) t -> g j p t", g=PASSES, p=P, j=PACK)
        row_pairs = xT.rearrange("(g p u e) t -> g u p (e t)", g=PASSES, p=P, u=2, e=2)

        def cols(first, count):
            return slice(first // PER_COL, (first + count) // PER_COL)

        def load_row(g, j):
            row = keep.tile([P, T], F32, name=f"row{g}{j}", align_bytes=64)
            nc.sync.dma_start(out=row[:], in_=rows[g, j])
            return row[:]

        def gather_woven(woven, j, row, first, count):
            slot = woven.rearrange("p (s j) -> p s j", j=PACK)[:, :, j]
            nc.vector.tensor_copy(slot, row.indirect(picks[:, cols(first, count)]))

        def gather_plane(plane, row, first, count):
            nc.scalar.activation(plane, row.indirect(picks[:, cols(first, count)]), COPY)

        def weave(woven, planes, lo, hi, copy=nc.vector.tensor_copy):
            walk = LINE // (4 if planes.dtype == F32 else 2)
            copy(
                woven.rearrange("p (c i j) -> p c j i", i=walk, j=PACK)[:, :, lo:hi, :],
                planes[:, lo:hi, :].rearrange("p j (c i) -> p c j i", i=walk),
            )

        def quantise(codes, scales, woven):
            nc.vector.quantize_mx(out=codes.bitcast(FP8X4), scales=scales, in_=woven)

        woven0 = keep.tile([P, PACK * S], BF16, name="woven0", align_bytes=64)
        planes0 = keep.tile([P, PACK, S - DIRECT], F32, name="planes0", align_bytes=64)
        codes0 = keep.tile([P, S], U32, name="codes0", align_bytes=64)
        scales0 = keep.tile([P, S], U8, name="scales0", align_bytes=64)
        pair = keep.tile([P, 2 * T], F32, name="pair", align_bytes=64)
        nc.sync.dma_start(out=pair[:], in_=row_pairs[0, 0])
        nc.sync.dma_start(picks[:], offs)
        for j in range(PACK):
            row = pair[:, j * T : (j + 1) * T] if j < 2 else load_row(0, j)
            gather_woven(woven0[:, 0 : PACK * DIRECT], j, row, 0, DIRECT)
            gather_plane(planes0[:, j, :], row, DIRECT, S - DIRECT)
        weave(woven0[:, PACK * DIRECT : PACK * S], planes0[:], 0, PACK)
        quantise(codes0[:], scales0[:], woven0[:])

        woven_a = keep.tile([P, PACK * PIECE], BF16, name="woven_a", align_bytes=64)
        woven_bc = keep.tile([P, PACK * 2 * PIECE], BF16, name="woven_bc", align_bytes=64)
        woven_b, woven_c = woven_bc[:, 0 : PACK * PIECE], woven_bc[:, PACK * PIECE :]
        planes1 = keep.tile([P, PACK, 3 * PIECE], BF16, name="planes1", align_bytes=64)
        planes = {first: planes1[:, :, first - B : first - B + PIECE] for first in (B, C, D)}
        for j in range(PACK):
            row = load_row(1, j)
            gather_woven(woven_a[:], j, row, A, PIECE)
            if j < PACK - 1:
                gather_plane(planes1[:, j, :], row, B, 3 * PIECE)
            else:
                nc.vector.tensor_copy(planes[D][:, j, PIECE - SPARE :], row.indirect(picks[:, cols(S - SPARE, SPARE)]))
                for first in (B, C, D):
                    count = min(PIECE, S - SPARE - first)
                    gather_plane(planes[first][:, j, 0:count], row, first, count)
            if j == 1:
                weave(woven_bc[:], planes1[:, :, 0 : 2 * PIECE], 0, 2)

        w_words = keep.tile([P, PASSES, 2 * N], U8, name="w_words", align_bytes=64)
        for g in range(PASSES):
            nc.sync.dma_start(out=w_words[:, g, :].bitcast(I32), in_=w1_words.bitcast(I32)[g])
        for q in range(4):
            nc.sync.dma_start(
                out=w_scales[32 * q : 32 * q + 4].bitcast(I32),
                in_=w1_scales.bitcast(I32)[:, 4 * q : 4 * q + 4, :].rearrange("g r n -> r g n"),
            )
        gates = keep.tile([P, S], F32, name="gates")
        nc.sync.dma_start(out=gates[:, 0:PIECE], in_=gate[:, 0:PIECE])
        nc.sync.dma_start(places[:], dst)
        for first, count in ((B, HALF), (B + HALF, HALF), (C, HALF), (C + HALF, HALF), (D, PIECE)):
            nc.sync.dma_start(out=gates[:, first : first + count], in_=gate[:, first : first + count])

        pass1 = {}

        def quantise1(first, count, woven, pool=keep, **place):
            codes = pool.tile([P, count], U32, name=f"codes1_{first}", align_bytes=64, **place)
            scales = keep.tile([P, count], U8, name=f"scales1_{first}", align_bytes=64)
            quantise(codes[:], scales[:], woven)
            for lo in range(0, count, PIECE):
                n = min(count, PIECE)
                pass1[first + lo] = (codes[:, lo : lo + n], scales[:, lo : lo + n])

        def group(y, b, steps, bank):
            count = sum(n for first, n in steps)
            acc = psum.tile([P, count], F32, name=f"acc{steps[0][0]}_{b}", tag=f"bank{bank}")
            calls = [(0, steps[0][0], count)] + [(1, first, n) for first, n in steps]

            def matmul(i):
                g, first, n = calls[i]
                codes, scales = (codes0[:, first : first + n], scales0[:, first : first + n]) if g == 0 else pass1[first]
                lo = first - steps[0][0]
                nc.tensor.matmul_mx(
                    out=acc[:, lo : lo + n],
                    lhsT=w_words[:, g, 2 * P * b : 2 * P * (b + 1)].bitcast(FP4X4),
                    lhsT_scale=w_scales[:, g, P * b : P * (b + 1)],
                    rhs=codes.bitcast(FP8X4),
                    rhs_scale=scales,
                    start=(i == 0),
                    stop=(i == len(calls) - 1),
                )

            def rest():
                for i in range(1, len(calls)):
                    matmul(i)
                nc.scalar.activation(y, acc[:], GELU)

            matmul(0)
            return rest

        ys = [keep.tile([P, S], F32, name=f"y{b}") for b in range(BLOCKS)]
        z1 = keep.tile([P, D], F32, name="z1")

        def gelu_piece(b, first, bank):
            group(ys[b][:, first : first + PIECE], b, [(first, PIECE)], bank)()

        def weigh(z, b, first, count=PIECE):
            nc.vector.tensor_tensor(z, ys[b][:, first : first + count], gates[:, first : first + count], MULT)

        def weigh1(first):
            weigh(z1[:, first : first + PIECE], 1, first)

        def scatter_on_scalar(first):
            nc.scalar.activation(windows[1][:].indirect(places[:, cols(first, PIECE)]), z1[:, first : first + PIECE], COPY)

        def scatter_on_vector(b, first, count=PIECE):
            weigh(windows[b][:].indirect(places[:, cols(first, count)]), b, first, count)

        quantise1(0, HALF, woven_a[:, 0 : PACK * HALF])
        quantise1(HALF, HALF, woven_a[:, PACK * HALF :], shared, offset=0)
        weave(woven_b, planes[B], 2, PACK)
        weave(woven_c, planes[C], 2, PACK)
        quantise1(B, PIECE, woven_b)
        quantise1(C, PIECE, woven_c)
        lead = [
            group(ys[0][:, 0:HALF], 0, [(0, HALF)], 0),
            group(ys[0][:, HALF:PIECE], 0, [(HALF, HALF)], 1),
            group(ys[1][:, 0:PIECE], 1, [(0, HALF), (HALF, HALF)], 2),
        ]
        for rest in lead:
            rest()
        scatter_on_vector(0, A)
        weigh1(A)
        woven_d = shared.tile([P, PACK * PIECE], BF16, name="woven_d", align_bytes=64, offset=0)
        weave(woven_d[:], planes[D], 0, PACK, nc.scalar.copy)
        gelu_piece(1, B, 4)
        gelu_piece(0, B, 3)
        gelu_piece(0, C, 5)
        gelu_piece(1, C, 6)
        scatter_on_scalar(A)
        quantise1(D, PIECE, woven_d[:])
        weigh1(B)
        scatter_on_vector(0, B)
        weigh1(C)
        gelu_piece(0, D, 7)
        scatter_on_scalar(B)
        gelu_piece(1, D, 0)
        scatter_on_vector(0, C, 2 * PIECE)
        scatter_on_scalar(C)
        scatter_on_vector(1, D)

        for b in range(BLOCKS):
            nc.sync.dma_start(out=out[P * b : P * (b + 1), :], in_=windows[b][:])
